import numpy as np, ml_dtypes
CORES = [78,86,94,102,110,118]
N = 6
BF = ml_dtypes.bfloat16
V, M, L, P, TV, HS = 4096, 1024, 256, 16, 5, (1, 2, 3, 5, 8)
def pushed(ls, s, n):
    return np.take_along_axis(ls.reshape(N, 8, 16 * M), (s & 15) * M + (((s * s >> 5) + s + 77 * n) & (M - 1)), 2)
def parts(rng):
    kd = rng.permutation(np.arange(V) & 3); pool = np.argsort(kd, kind="stable").reshape(4, V >> 2)
    own = np.where(rng.random((N, 8, V)) < 0.02, rng.integers(0, 4, (N, 8, V)), kd); proto = rng.integers(0, 16, (N, 8, 16, 4))
    x = np.clip(np.take_along_axis(proto, own[:, :, None], 3) + rng.integers(-1, 2, (N, 8, 16, V)), 0, 15)
    ls = rng.integers(0, V, (N, 8, 16, M)); s = rng.integers(0, 4096, (N, 8, L))
    n = np.where(rng.random((N, 8, L)) < 0.5, rng.integers(15, 17, (N, 8, L)), rng.integers(0, 17, (N, 8, L)))
    return kd, pool, x, ls, s, n, rng.integers(10, 30, (N, 8)), rng.integers(0, 256, (N, 8, 16))
def spell(rng, ls, s, n, kd, pool, p):
    a = kd[pushed(ls, s, n)]; b = (a + rng.integers(1, 4, a.shape)) & 3; j = np.arange(1, 17)[:, None]; sh = (N, 8, 16, L)
    k = np.where(j % np.maximum(p, 1)[:, :, None] == 0, a[:, :, None], b[:, :, None])
    cut = np.maximum(2 * p, rng.integers(0, 17, p.shape))[:, :, None]
    k = np.where((p[:, :, None] == 0) | (j >= cut), rng.integers(0, 4, sh), k)
    return pool[k, rng.integers(0, V >> 2, sh)]
def two(a, b, p):
    j = np.arange(1, 17)[:, None]; q = np.where(p == 0, 99, p)[:, :, None]
    return np.where(j % q == 0, a[:, :, None], b[:, :, None])
def pack(x, ls, w, s, n, th, wt):
    w = np.where(np.arange(16)[:, None] < n[:, :, None, :], w, 0)
    return {"x": np.ascontiguousarray(x.reshape(N, 128, V)).astype(np.float32).astype(BF), "ls": np.ascontiguousarray(ls.reshape(N, 128, M)).astype(np.int32),
            "wd": np.ascontiguousarray(w.reshape(N, 128, L)).astype(np.int32), "nl": n.astype(np.int32), "sd": s.astype(np.int32),
            "th": np.ascontiguousarray(th.reshape(N, 8, 1)).astype(np.int32), "wt": np.ascontiguousarray(wt.reshape(N, 128, 1)).astype(np.int32)}
def setup_inputs(rng):
    kd, pool, x, ls, s, n, th, wt = parts(rng); p = rng.choice(np.array((0, 0) + HS), (N, 8, L))
    return pack(x, ls, spell(rng, ls, s, n, kd, pool, p), s, n, th, wt)
def setup_inputs_corners(rng):
    kd, pool, x, ls, s, n, th, wt = parts(rng); sh = (N, 8, L)
    ls = np.where(rng.random(ls.shape) < 0.2, rng.choice(np.array([0, V - 1]), ls.shape), ls)
    edge = np.array(sorted({0, 1, 15, 16} | {2 * h - 2 for h in HS} | {2 * h - 1 for h in HS})); p = rng.choice(np.array(HS), sh); u = rng.random(sh)
    n = np.where(u < 0.4, 2 * p - 2, np.where(u < 0.7, 2 * p - 1, rng.choice(edge, sh)))
    n[0, 0] = 0; n[N - 1, 7] = 16; n[:, 3] = rng.choice(np.array([0, 16]), (N, L))
    s = np.where(rng.random(sh) < 0.3, rng.choice(np.array([0, 15, 16, 4095]), sh), s)
    th = rng.choice(np.array([0, 1, 20, 240]), (N, 8)); wt = rng.choice(np.array([0, 1, 255]), (N, 8, 16))
    p[N - 1, 7] = 8; th[N - 1, 7] = 0
    c = int(rng.integers(1, N - 1))
    x[c] = 8 * (np.arange(V) & 1) + rng.integers(0, 3, (8, 16, V)); th[c] = 8; th[c - 1] = 240
    ls[c - 1] |= 1; ls[c] -= ls[c] & 1
    n[c - 1] = 0; n[c] = np.maximum(n[c], 1); n[c, 7, L - 1] = 0
    a = pushed(ls, s, n); u = rng.integers(0, 4, sh); own = P * np.arange(L) + rng.integers(0, P, sh)
    b = np.where(u == 0, 0, np.where(u == 1, V - 1, np.where(u == 2, own, rng.integers(0, V, sh))))
    w = two(a, b, p); w[c, :, 0] = a[c]
    return pack(x, ls, w, s, n, th, wt)
def setup_inputs_ties(rng):
    kd, pool, x, ls, s, n, th, wt = parts(rng); sh = (N, 8, L); half = V >> 3
    th = rng.integers(16, 61, (N, 8)); val = np.stack([0 * th, th, th + 1, 2 * th + 1], -1)
    loose = np.ones(V, np.int64); loose[pool[:, :half]] = 0
    e = val[:, :, kd] + loose * rng.integers(0, 17, (N, 8, V)); x = (e[:, :, None] + np.arange(16)[:, None]) >> 4
    ls = np.where(rng.random(ls.shape) < 0.8, pool[rng.integers(0, 4, ls.shape), rng.integers(0, half, ls.shape)], ls)
    p = rng.choice(np.array(HS), sh); a = kd[pushed(ls, s, n)]; b = np.array([3, 3, 0, 0])[a]
    c = np.where(rng.random(sh) < 0.6, np.array([1, 0, 3, 2])[a], np.array([2, 3, 0, 1])[a])
    k = np.where(np.arange(1, 17)[:, None] == p[:, :, None], c[:, :, None], two(a, b, p))
    return pack(x, ls, pool[k, rng.integers(0, half, k.shape)], s, n, th, wt)
def setup_inputs_again(rng):
    kd, pool, x, ls, s, n, th, wt = parts(rng)
    few = np.concatenate([np.arange(4 * P), V - 4 * P + np.arange(4 * P)])
    x = np.clip(rng.integers(0, 16, (N, 8, 16, 1)) + rng.integers(-3, 4, (N, 8, 16, V)), 0, 15); th = rng.integers(24, 44, (N, 8))
    ls = few[rng.integers(0, 8 * P, ls.shape)]; w = few[rng.integers(0, 8 * P, (N, 8, 16, L))]
    q = int(rng.integers(0, N)); n[q] = np.maximum(n[q], 1); w[q, :, 0] = pushed(ls, s, n)[q]
    return pack(x, ls, w, s, n, th, wt)
def setup_inputs_spread(rng):
    sh = (N, 8, L)
    x = np.minimum((np.exp2(4 * rng.random((N, 8, 1, V))) * rng.random((N, 8, 16, V))).astype(np.int64), 15)
    ls = np.minimum((V * rng.random((N, 8, 16, M)) * np.sqrt(rng.random((N, 8, 16, M)))).astype(np.int64), V - 1)
    w = np.minimum((np.exp2(np.log2(V) * rng.random((N, 8, 16, L)))).astype(np.int64), V - 1)
    s = np.where(rng.random(sh) < 0.5, rng.integers(0, 4096, sh), np.minimum(np.exp2(12 * rng.random(sh)).astype(np.int64), 4095))
    wt = np.minimum(np.exp2(8 * rng.random((N, 8, 16))).astype(np.int64) - 1, 255)
    return pack(x, ls, w, s, rng.integers(0, 17, sh), rng.integers(0, 241, (N, 8)), wt)
def setup_inputs_ends(rng):
    sh = (N, 8, L)
    u = rng.integers(0, 3, (N, 8, 1, V)); x = 15 * np.where(u == 2, rng.integers(0, 2, (N, 8, 16, V)), u)
    x[:, 1:7:2, :, 0] = 0; x[:, 1:7:2, :, V - 1] = 15; x[:, 7, :, 0] = 0; x[:, 7, :, V - 1] = 15; x[:, 0, :, 0] = 15; x[:, 0, :, V - 1] = 0
    ls = (V - 1) * rng.integers(0, 2, (N, 8, 16, M)); s = 4095 * rng.integers(0, 2, sh); n = 16 * (rng.random(sh) < 0.75).astype(np.int64)
    th = 240 * rng.integers(0, 2, (N, 8)); th[:, 7] = 0; th[:, 6] = 240
    wt = 255 * rng.integers(0, 2, (N, 8, 16)); wt[:, 7] = 255; wt[:, 0] = 0
    p = rng.choice(np.array((0,) + HS), sh)
    for i, k in ((0, 0), (1, 8), (7, 0), (10, 8), (L - 2, 8), (L - 1, 0)):
        s[:, 7, i] = 4095; n[:, 7, i] = 16; p[:, 7, i] = k
    ls[:, 7, 15, ((4095 * 4095 >> 5) + 4095 + 77 * 16) & (M - 1)] = V - 1
    a = pushed(ls, s, n)
    return pack(x, ls, two(a, V - 1 - a, p), s, n, th, wt)
def check_inputs(d):
    bad = []
    for k, lo, hi in (("x", 0, 15), ("ls", 0, V - 1), ("wd", 0, V - 1), ("nl", 0, 16), ("sd", 0, 4095), ("th", 0, 240), ("wt", 0, 255)):
        v = np.asarray(d[k]).astype(np.float64)
        if not np.all((v >= lo) & (v <= hi)): bad.append("range of " + k)
        if not np.all(v == np.floor(v)): bad.append("whole numbers in " + k)
    w = np.asarray(d["wd"]).reshape(N, 8, 16, L); n = np.asarray(d["nl"]).reshape(N, 8, 1, L)
    if np.any((np.arange(16)[:, None] >= n) & (w != 0)): bad.append("empty rows of wd")
    return bad
def reference(x, ls, wd, nl, sd, th, wt):
    X = x.astype(np.float32).astype(np.int32).reshape(N, 8, 16, V); tab = ls.astype(np.int64).reshape(N, 8, 16 * M)
    w = wd.astype(np.int64).reshape(N, 8, 16, L); n = nl.astype(np.int64); s = sd.astype(np.int64)
    lim = th.astype(np.int64).reshape(N, 8, 1, 1); wgt = wt.astype(np.int64).reshape(N, 8, 16, 1)
    A = np.zeros(N, np.int64); row = np.arange(16)[:, None]
    for t in range(TV):
        new = np.take_along_axis(tab, (s & 15) * M + (((s * s >> 5) + s + 77 * n) & (M - 1)), 2)
        w = np.concatenate([new[:, :, None], w[:, :, :15]], axis=2); n = np.minimum(n + 1, 16)
        G = np.take_along_axis(X, w.reshape(N, 8, 1, 16 * L), 3).reshape(N, 8, 16, 16, L)
        bound = lim + (A & 15).reshape(N, 1, 1, 1); h = np.zeros((N, 8, L), np.int64)
        for k in HS:
            D = np.add.reduce(np.abs(G[:, :, :, :k] - G[:, :, :, k:2 * k]), axis=2)
            h = np.where((h == 0) & (2 * k <= n) & np.all(D <= bound, axis=2), k, h)
        hit = h > 0
        z = np.maximum.reduce(np.where(row < h[:, :, None, None, :], G, 0), axis=3)
        tot = np.add.reduce(wgt * np.where(hit[:, :, None], z, G[:, :, :, 0]), axis=2)
        s = np.where(hit, tot + h, 5 * s + tot) & 4095
        at = row + h[:, :, None, :]
        w = np.where(at < 16, np.take_along_axis(w, np.minimum(at, 15), 2), 0); n = n - h
        col = np.roll(P * np.arange(L) + (s & (P - 1)), 1, axis=0)[:, :, None]
        old = np.take_along_axis(X, col, 3)
        val = np.where(np.roll(hit, 1, axis=0)[:, :, None], (old + np.roll(z, 1, axis=0)) >> 1, old)
        np.put_along_axis(X, col, val.astype(np.int32), 3)
        A = np.add.reduce(hit.astype(np.int64).reshape(N, 8 * L), axis=1)
        if t < TV - 1:
            by = 1 + (t + 1) // N - t // N
            w, n, s = [np.roll(np.roll(v, 1, axis=0), by, axis=1) for v in (w, n, s)]
    return {"yx": X.reshape(N, 128, V).astype(np.float32).astype(BF), "yw": w.reshape(N, 128, L).astype(np.float32), "yn": n.astype(np.float32), "ys": s.astype(np.float32)}

@@ -1,0 +1,544 @@
+from concourse.mybir import AluOpType as A, AxisListType, ActivationFunctionType as F
+
+HS = (8, 5, 3, 2, 1)
+BASE = {8: 1, 5: 9, 3: 14, 2: 17, 1: 19}
+SLOT = {1: 0, 2: 1, 3: 2, 5: 4, 8: 7, 0: 5}
+TV = 5
+PAIRS = [(h, j) for h in (5, 3, 2, 1) for j in range(h)]
+
+SCRATCH = {
+    "X": ("sbuf", [128, 8192], "bfloat16"), "LS": ("sbuf", [128, 1024], "int32"), "LSN": ("sbuf", [128, 1024], "int32"),
+    "SH": ("sbuf", [128, 2048], "float32"), "GL": ("sbuf", [128, 2048], "bfloat16"), "GH": ("sbuf", [128, 2048], "bfloat16"),
+    "D8": ("sbuf", [128, 2048], "bfloat16"), "DL": ("sbuf", [128, 11 * 256], "bfloat16"), "ZC": ("sbuf", [128, 2048], "bfloat16"),
+    "ZR": ("sbuf", [128, 2048], "bfloat16"), "NEG": ("sbuf", [128, 256], "bfloat16"),
+    "M1S": ("sbuf", [128, 5 * 288], "bfloat16"), "M1R": ("sbuf", [128, 5 * 288], "bfloat16"),
+    "MLS": ("sbuf", [128, 5 * 16], "uint16"), "MLR": ("sbuf", [128, 5 * 16], "uint16"),
+    "MNS": ("sbuf", [128, 5 * 32], "float32"), "MNR": ("sbuf", [128, 5 * 32], "float32"),
+    "W2": ("sbuf", [128, 5 * 256], "float32"), "W2R": ("sbuf", [128, 5 * 256], "float32"),
+    "LF": ("sbuf", [128, 5 * 256], "float32"), "LFR": ("sbuf", [128, 5 * 256], "float32"),
+    "IDB": ("sbuf", [128, 128], "bfloat16"), "NIB": ("sbuf", [128, 128], "bfloat16"), "IDF": ("sbuf", [128, 128], "float32"),
+    "ONE": ("sbuf", [128, 128], "bfloat16"), "ONEF": ("sbuf", [128, 128], "float32"), "ROW0": ("sbuf", [128, 128], "float32"),
+    "RA": ("sbuf", [128, 512], "float32"), "ME": ("sbuf", [128, 288], "float32"),
+    "KB": ("sbuf", [128, 8], "bfloat16"), "KF": ("sbuf", [128, 8], "float32"), "K256": ("sbuf", [128, 8], "bfloat16"),
+    "K2": ("sbuf", [128, 8], "bfloat16"), "KN": ("sbuf", [128, 8], "bfloat16"), "WTB": ("sbuf", [128, 8], "bfloat16"),
+    "CP": ("sbuf", [128, 640], "bfloat16"), "DB": ("sbuf", [128, 160], "bfloat16"), "RB": ("sbuf", [128, 160], "bfloat16"),
+    "D0": ("sbuf", [128, 160], "bfloat16"), "C2": ("sbuf", [128, 160], "bfloat16"), "THR": ("sbuf", [128, 320], "float32"),
+    "E": ("sbuf", [128, 320], "bfloat16"), "SC2": ("sbuf", [128, 320], "bfloat16"),
+    "EK": ("sbuf", [128, 288], "bfloat16"), "EC": ("sbuf", [128, 288], "float32"), "RS": ("sbuf", [128, 288], "bfloat16"),
+    "EV": ("sbuf", [128, 256], "bfloat16"), "EL": ("sbuf", [128, 256], "float32"),
+    "LS9": ("sbuf", [128, 18], "uint16"), "LK9": ("sbuf", [128, 18], "uint16"), "LU": ("sbuf", [128, 16], "uint16"), "ROT": ("sbuf", [128, 2], "uint16"),
+    "BI": ("sbuf", [128, 16], "float32"), "B8": ("sbuf", [128, 16], "bfloat16"), "B16": ("sbuf", [128, 16], "bfloat16"),
+    "II": ("sbuf", [128, 128], "int32"), "IM": ("sbuf", [128, 288], "int32"), "IG": ("sbuf", [128, 8], "int32"), "I20": ("sbuf", [128, 160], "int32"),
+    "IP": ("sbuf", [128, 4], "int32"), "IK": ("sbuf", [128, 16], "int32"), "I9": ("sbuf", [128, 18], "int32"), "IU": ("sbuf", [128, 16], "int32"),
+    "P15": ("sbuf", [128, 1], "float32"), "PB": ("sbuf", [128, 2], "float32"), "P15I": ("sbuf", [128, 4], "int32"),
+    "SDI": ("sbuf", [8, 256], "int32"), "NLI": ("sbuf", [8, 256], "int32"), "SDF": ("sbuf", [8, 256], "float32"), "NLF": ("sbuf", [8, 256], "float32"),
+    "WTI": ("sbuf", [128, 1], "int32"), "WTF": ("sbuf", [128, 1], "float32"), "THI": ("sbuf", [128, 1], "int32"), "THF": ("sbuf", [128, 1], "float32"),
+    "WI": ("sbuf", [128, 256], "int32"), "LH": ("sbuf", [128, 256], "uint16"), "L1": ("sbuf", [128, 16], "uint16"), "L2": ("sbuf", [128, 16], "uint16"),
+    "LLU": ("sbuf", [128, 16], "uint16"), "CL": ("sbuf", [128, 16], "uint16"), "KBI": ("sbuf", [128, 16], "int32"),
+    "N0": ("sbuf", [128, 16], "float32"), "N1": ("sbuf", [128, 16], "float32"), "NP": ("sbuf", [128, 16], "float32"),
+    "NH": ("sbuf", [128, 16], "float32"), "H": ("sbuf", [128, 16], "float32"), "H1": ("sbuf", [128, 16], "float32"),
+    "S5": ("sbuf", [128, 16], "float32"), "AD": ("sbuf", [128, 16], "float32"), "DU": ("sbuf", [128, 16], "int32"),
+    "SUM": ("sbuf", [128, 16], "int32"), "V15": ("sbuf", [128, 16], "int32"), "VV": ("sbuf", [128, 16], "int32"), "SI": ("sbuf", [128, 16], "int32"),
+    "S15": ("sbuf", [128, 16], "int32"), "T1": ("sbuf", [128, 16], "int32"), "T2": ("sbuf", [128, 16], "int32"), "U": ("sbuf", [128, 16], "int32"), "CI": ("sbuf", [128, 16], "int32"),
+    "MK": ("sbuf", [128, 256], "float32"), "MM": ("sbuf", [128, 256], "float32"), "LW": ("sbuf", [128, 16], "float32"),
+    "XT": ("sbuf", [128, 256], "bfloat16"), "XU": ("sbuf", [128, 256], "bfloat16"),
+    "NS": ("sbuf", [128, 1], "float32"), "AI": ("sbuf", [128, 1], "int32"), "BC": ("sbuf", [128, 1], "float32"), "AJ": ("sbuf", [128, 1], "int32"),
+    "YW": ("sbuf", [128, 256], "float32"), "YN": ("sbuf", [8, 256], "float32"), "YS": ("sbuf", [8, 256], "float32"), "SF": ("sbuf", [128, 16], "float32"),
+    "PG": ("psum", [128, 2048], "float32"), "B4": ("psum", [128, 512], "float32"), "B5": ("psum", [128, 512], "float32"),
+    "PD0": ("psum", [128, 512], "float32"), "PD1": ("psum", [128, 512], "float32"),
+}
+_ARR = ["%s%d" % (n, t) for n in ("M1", "ML", "MN", "W2", "LF") for t in range(TV)] + ["LS"]
+_DMA = ["small", "sm2", "ls", "wd", "x", "sh", "sh2", "oyx", "oyw", "oyn"]
+SEMAPHORES = ["qv", "qa", "qp", "qg", "loc"] + ["r" + n for n in _ARR] + ["d" + n for n in _DMA]
+
+
+def rank_program(g, core, T, topo):
+    rank = T.rank_of(core)
+    if rank is None:
+        return
+    N = len(T.cores)
+    nxt, nx2, prv = T.cores[(rank + 1) % N], T.cores[(rank + 2) % N], T.cores[(rank - 1) % N]
+    V, P, S = g.vector, g.tensor, g.scalar
+    Q = {"v": V, "a": S, "p": P, "g": g, "s": g.sync}
+
+    tot = {}
+    known = {q: {} for q in Q}
+    lastw, readers, banks, ops = {}, {}, {}, []
+
+    def need(q, deps):
+        for o in sorted(deps, reverse=True):
+            sem, val, snap, dma = ops[o]
+            if known[q].get(sem, 0) >= val:
+                continue
+            if dma:
+                val = tot[sem]
+            Q[q].wait_ge(T.sem[sem], val)
+            for s_, v_ in snap.items():
+                known[q][s_] = max(known[q].get(s_, 0), v_)
+            known[q][sem] = val
+
+    def deps_of(q, r, w, b):
+        d = set()
+        for k in r:
+            d.update(lastw.get(k, ()))
+        for k in w:
+            d.update(lastw.get(k, ()))
+            d.update(readers.get(k, ()))
+        for k in b:
+            d.update(o for q_, o in banks.get(k, {}).items() if q_ != q)
+        return d
+
+    def note(q, sem, inc, r, w, b, dma=False):
+        tot[sem] = tot.get(sem, 0) + inc
+        o = len(ops)
+        ops.append((sem, tot[sem], dict(known[q]) if q else {}, dma))
+        for k in w:
+            lastw[k] = [o]
+            readers[k] = []
+        for k in r:
+            readers.setdefault(k, []).append(o)
+        for k in b:
+            banks.setdefault(k, {})[q] = o
+        return o
+
+    def run(q, fn, *a, r="", w="", b="", **k):
+        r, w, b = r.split(), w.split(), b.split()
+        need(q, deps_of(q, r, w, b))
+        sem = "q" + q
+        fn(*a, **k).then_inc(T.sem[sem], 1)
+        note(q, sem, 1, r, w, b)
+
+    def v(fn, *a, **k):
+        run("v", fn, *a, **k)
+
+    def act(out, in_, func=F.Copy, r="", w="", b="", **k):
+        run("a", S.activation, out, in_, func, r=r, w=w, b=b, **k)
+
+    def mm(out, l, rh, start=True, stop=True, r="", w="", b=""):
+        r, w, b = r.split(), w.split(), b.split()
+        need("p", deps_of("p", r, [], b))
+        P.matmul(out, l, rh, start, stop).then_inc(T.sem.qp, 1)
+        note("p", "qp", 1, r, w, b)
+
+    def dma(sem, out, in_, r="", w=""):
+        r, w = r.split(), w.split()
+        need("s", deps_of("s", r, w, []))
+        g.sync.dma_start(out, in_).then_inc(T.sem["d" + sem], 16)
+        note("s", "d" + sem, 16, r, w, [], True)
+
+    def send(name, dst, out, in_, r=""):
+        r = r.split()
+        need("g", deps_of("g", r, [], []))
+        rid, pid = topo.addr(dst)[:2]
+        g.remote_dma(out, in_, T.sem["r" + name], T.sem.loc, pid, rid, topo.mask(core, dst))
+        note("g", "loc", len(topo.engines(core, dst)), [], [], [])
+
+    def arrive(name, src, key):
+        n = len(topo.engines(src, core))
+        tot["r" + name] = n
+        lastw[key] = [len(ops)]
+        ops.append(("r" + name, n, {}, False))
+
+    p2 = T.cores[(rank - 2) % N]
+    for t in range(TV):
+        arrive("M1%d" % t, prv, "M1R%d" % t)
+        arrive("ML%d" % t, prv, "MLR%d" % t)
+        if t < 4:
+            arrive("MN%d" % t, prv, "MNR%d" % t)
+            arrive("W2%d" % t, prv, "W2R%d" % t)
+        arrive("LF%d" % t, prv if t in (0, 4) else p2, "LFR%d" % t)
+    arrive("LS", nxt, "LSN")
+
+    v(V.memset, T.THI[:], 0, w="THI")
+    dma("small", T.SDI[:], T.sd[:], w="SDI")
+    dma("small", T.NLI[:], T.nl[:], w="NLI")
+    dma("ls", T.LS[:], T.ls[:], w="LS")
+    dma("wd", T.WI[1:128, :], T.wd[0:127, :], w="WIa")
+    dma("wd", T.WI[0:1, :], T.wd[0:1, :], w="WIb")
+    dma("sm2", T.THI[0:128:16, :], T.th[:], w="THI")
+    dma("sm2", T.WTI[:], T.wt[:], w="WTI")
+    dma("x", T.X[:, 0:4096], T.x[:], w="X")
+
+    def iota(out, pat, base, cm, key):
+        run("g", g.iota, out, pat, base, cm, w=key)
+    iota(T.II[:], [[-1, 128]], 0, 1, "II")
+    iota(T.IG[:], [[-16, 8]], 0, 1, "IG")
+    iota(T.IP[:], [[0, 4]], 0, 1, "IP")
+    iota(T.I9[:, 1:9], [[1, 8]], 0, 0, "I9a")
+    iota(T.I9[:, 10:18], [[1, 8]], 8, 0, "I9b")
+    iota(T.I9[:, 0:1], [[1, 1]], 7, 0, "I9c")
+    iota(T.I9[:, 9:10], [[1, 1]], 15, 0, "I9d")
+    iota(T.IM[:], [[0, 18], [-1, 16]], 0, 1, "IM")
+    iota(T.IU[:], [[1, 16]], 0, 0, "IU")
+    iota(T.IK[:], [[16, 16]], 0, 0, "IK")
+    iota(T.I20[:], [[-16, 8], [0, 20]], 0, 1, "I20")
+    v(V.tensor_scalar, T.IDF[:], T.II[:], 0, None, A.is_equal, r="II", w="IDF")
+    v(V.tensor_copy, T.SDF[:], T.SDI[:], r="SDI", w="SDF")
+    v(V.tensor_copy, T.NLF[:], T.NLI[:], r="NLI", w="NLF")
+    for hf in range(2):
+        mm(T.B4[:, 8 * hf:8 * hf + 8], T.SDF[:, 128 * hf:128 * hf + 128], T.IDF[0:8, 0:8], r="SDF IDF", w="B4sd", b="B4")
+    for hf in range(2):
+        mm(T.B4[:, 16 + 8 * hf:24 + 8 * hf], T.NLF[:, 128 * hf:128 * hf + 128], T.IDF[0:8, 0:8], r="NLF IDF", w="B4sd", b="B4")
+    v(V.tensor_scalar, T.IG[:], T.IG[:], 4, None, A.arith_shift_right, r="IG", w="IG")
+    v(V.tensor_scalar, T.KB[:], T.IG[:], 0, None, A.is_equal, r="IG", w="KB")
+    v(V.tensor_scalar, T.KF[:], T.IG[:], 0, None, A.is_equal, r="IG", w="KF")
+    v(V.tensor_scalar, T.IM[:], T.IM[:], 15, None, A.bitwise_and, r="IM", w="IM")
+    v(V.tensor_scalar, T.ME[:], T.IM[:], 0, None, A.is_equal, r="IM", w="ME")
+    v(V.tensor_copy, T.LS9[:], T.I9[:], r="I9a I9b I9c I9d", w="LS9")
+    v(V.tensor_scalar, T.LK9[:], T.I9[:], 20, 19, A.mult, A.add, r="I9a I9b I9c I9d", w="LK9")
+    v(V.tensor_copy, T.LU[:], T.IU[:], r="IU", w="LU")
+    v(V.tensor_copy, T.SI[:], T.B4[:, 0:16], r="B4sd", w="SI", b="B4")
+    v(V.tensor_copy, T.N0[:], T.B4[:, 16:32], r="B4sd", w="N0", b="B4")
+    v(V.tensor_scalar, T.P15I[:, 0:1], T.IP[:, 0:1], 15, None, A.bitwise_and, r="IP", w="P15I")
+    v(V.tensor_copy, T.P15[:], T.P15I[:, 0:1], r="P15I", w="P15")
+    v(V.tensor_copy, T.IDB[:], T.IDF[:], r="IDF", w="IDB")
+
+    def push1(ncol, nkey):
+        v(V.tensor_tensor, T.T1[:], T.SI[:], T.SI[:], A.mult, r="SI", w="T1")
+        v(V.tensor_scalar, T.U[:], ncol, 77, None, A.mult, r=nkey, w="U")
+        v(V.tensor_scalar, T.S15[:], T.SI[:], 15, None, A.bitwise_and, r="SI", w="S15")
+        v(V.tensor_scalar, T.T2[:], T.T1[:], 5, None, A.arith_shift_right, r="T1", w="T2")
+        v(V.tensor_tensor, T.U[:], T.U[:], T.SI[:], A.add, r="U SI", w="U")
+        v(V.tensor_tensor, T.T1[:], T.T2[:], T.U[:], A.add, r="T2 U", w="T1")
+        v(V.tensor_scalar, T.CI[:], T.T1[:], 1023, None, A.bitwise_and, r="T1", w="CI")
+        v(V.tensor_tensor, T.EC[:], T.CI[:].indirect(T.LS9[:]), T.ME[:], A.mult, r="CI LS9 ME", w="EC")
+        v(V.tensor_copy, T.RS[:], T.S15[:].indirect(T.LS9[:]), r="S15 LS9", w="RS")
+
+    def push2(sl):
+        for hf in range(2):
+            mm(T.PG[:, 8 * hf:8 * hf + 8], T.EC[:, 144 * hf + sl:144 * hf + sl + 128], T.KF[:], r="EC KF", w="pC", b="PG0")
+        for hf in range(2):
+            mm(T.PG[:, 512 + 128 * hf:640 + 128 * hf], T.RS[:, 144 * hf + sl:144 * hf + sl + 128], T.IDB[:], r="RS IDB", w="pR", b="PG1")
+
+    def push2b(ls):
+        v(V.tensor_copy, T.CL[:], T.PG[:, 0:16], r="pC", w="CL", b="PG0")
+        v(V.tensor_scalar, T.MK[:], T.PG[:, 512:768], T.P15[:], None, A.is_equal, r="pR P15", w="MK", b="PG1")
+        v(V.tensor_tensor, T.MM[:], T[ls][:].indirect(T.CL[:]), T.MK[:], A.mult, r=ls + " CL MK", w="MM")
+        for hf in range(2):
+            mm(T.PG[:, 1024 + 8 * hf:1032 + 8 * hf], T.MM[:, 128 * hf:128 * hf + 128], T.KF[:], r="MM KF", w="pW", b="PG2")
+        mm(T.PG[:, 1536:1792], T.ROW0[:], T.MM[:], r="MM ROW0", w="pF", b="PG3")
+
+    def push3(t):
+        v(V.tensor_copy, T.LW[:], T.PG[:, 1024:1040], r="pW", w="LW", b="PG2")
+        act(T.LF[:, 256 * t:256 * t + 256], T.PG[:, 1536:1792], r="pF", w="LF%d" % t, b="PG3")
+
+    def push4():
+        v(V.tensor_tensor, T.EL[:], T.LW[:].indirect(T.LU[:]), T.ME[:, 0:256], A.mult, r="LW LU ME", w="EL")
+        for hf in range(2):
+            mm(T.B5[:, 8 * hf:8 * hf + 8], T.EL[:, 128 * hf:128 * hf + 128], T.KF[:], r="EL KF", w="pL", b="B5")
+
+    push1(T.N0[:], "N0")
+    v(V.memset, T.ROW0[:], 0.0, w="ROW0")
+    v(V.tensor_copy, T.ROW0[:, 0:128:16], T.KF[:], r="KF", w="ROW0")
+    push2(16)
+    push2b("LS")
+    v(V.tensor_scalar, T.P15I[:, 1:2], T.IP[:, 0:1], 3, 1, A.arith_shift_right, A.bitwise_and, r="IP", w="P15b")
+    v(V.tensor_copy, T.PB[:, 1:2], T.P15I[:, 1:2], r="P15b", w="PB1")
+    v(V.tensor_scalar, T.PB[:, 0:1], T.P15I[:, 1:2], -1, 1, A.mult, A.add, r="P15b", w="PB0")
+    for b_ in range(2):
+        for w_ in range(2):
+            c = 128 * (2 * b_ + w_)
+            v(V.tensor_scalar, T.RA[:, c:c + 128], T.II[:], 8 * (b_ - w_), T.PB[:, b_:b_ + 1], A.is_equal, A.mult, r="II PB%d" % b_, w="RA%d%d" % (b_, w_))
+    v(V.tensor_copy, T.W2[:, 0:256], T.WI[:], r="WIa WIb", w="W20")
+    push3(0)
+    push4()
+    v(V.tensor_copy, T.LLU[:], T.B5[:, 0:16], r="pL", w="LLU", b="B5")
+    send("LF0", nxt, T.LFR[:, 0:256], T.LF[:, 0:256], r="LF0")
+    send("LS", prv, T.LSN[:], T.LS[:], r="LS")
+
+    def rearr(t):
+        w2 = 256 * t
+        for b_ in range(2):
+            for w_ in range(2):
+                c = 128 * (2 * b_ + w_)
+                mm(T.B4[:, 128 * b_:128 * b_ + 128], T.RA[:, c:c + 128], T.W2[:, w2 + w_:w2 + 256:2], w_ == 0, w_ == 1, r="W2%d RA%d%d" % (t, b_, w_), w="pH", b="B4")
+
+    def lists():
+        v(V.tensor_copy, T.LH[:], T.B4[:, 0:256], r="pH", w="LH", b="B4")
+
+    rearr(0)
+    lists()
+    v(V.tensor_copy, T.WTF[:], T.WTI[:], r="WTI", w="WTF")
+    v(V.tensor_copy, T.THF[:], T.THI[:], r="THI", w="THF")
+    v(V.tensor_scalar, T.WTB[:], T.KB[:], T.WTF[:], None, A.mult, r="KB WTF", w="WTB")
+    v(V.tensor_scalar, T.K2[:], T.KB[:], 2, None, A.mult, r="KB", w="K2")
+    v(V.tensor_scalar, T.KN[:], T.KB[:], -1, None, A.mult, r="KB", w="KN")
+    v(V.tensor_scalar, T.K256[:], T.KB[:], 256, None, A.mult, r="KB", w="K256")
+    v(V.tensor_scalar, T.DB[:], T.I20[:], 0, None, A.is_equal, r="I20", w="DB")
+    v(V.memset, T.CP[:], 0.0, w="CP")
+    for h in HS:
+        for k_, j in ((0, 0), (1, 1), (2, 2), (3, 0)):
+            if h > j and not (k_ == 3 and h == 8):
+                v(V.tensor_copy, T.CP[:, 160 * k_ + BASE[h] + j:160 * k_ + 160:20], T.KN[:], r="KN CP", w="CP%d%d" % (k_, h))
+    cpk = " CP " + " ".join("CP%d%d" % (k_, h) for k_ in range(4) for h in HS)
+    v(V.memset, T.ONE[:], 1.0, w="ONE")
+    v(V.tensor_scalar, T.NIB[:], T.IDB[:], -1, None, A.mult, r="IDB", w="NIB")
+    v(V.memset, T.ZR[:], 1.0, w="ZR")
+    v(V.memset, T.ZR[:, 0:2048:8], 0.0, w="ZR")
+    v(V.memset, T.D0[:], 1.0, w="D0")
+    for q_ in (0, 1, 9, 14, 17, 19):
+        v(V.memset, T.D0[:, q_:160:20], 0.0, r="D0", w="D0%d" % q_)
+    d0k = "D0 " + " ".join("D0%d" % q_ for q_ in (0, 1, 9, 14, 17, 19))
+    v(V.memset, T.C2[:], 0.0, w="C2")
+    for q_, c in ((0, -2.0), (8, 3.0), (13, 2.0), (16, 1.0), (18, 1.0)):
+        v(V.memset, T.C2[:, q_:160:20], c, r="C2", w="C2%d" % q_)
+    c2k = "C2 C20 C28 C213 C216 C218"
+    v(V.memset, T.THR[:], -1.0, w="THR")
+    v(V.memset, T.THR[:, 0:320:20], 1000.0, r="THR", w="THR0")
+    v(V.tensor_scalar, T.BI[:], T.IK[:], T.P15[:], None, A.add, r="IK P15", w="BI")
+    v(V.tensor_scalar, T.B8[:], T.BI[:], 8, None, A.mult, r="BI", w="B8")
+    v(V.tensor_scalar, T.B16[:], T.BI[:], 16, None, A.mult, r="BI", w="B16")
+    v(V.tensor_scalar, T.P15I[:, 2:3], T.P15I[:, 0:1], 8, None, A.bitwise_and, r="P15I", w="P15c")
+    v(V.tensor_scalar, T.P15I[:, 3:4], T.P15I[:, 0:1], -1, None, A.add, r="P15I", w="P15d")
+    v(V.tensor_scalar, T.P15I[:, 3:4], T.P15I[:, 3:4], 7, None, A.bitwise_and, r="P15d", w="P15d")
+    v(V.tensor_tensor, T.P15I[:, 2:3], T.P15I[:, 2:3], T.P15I[:, 3:4], A.add, r="P15c P15d", w="P15c")
+    v(V.tensor_copy, T.ROT[:, 0:1], T.P15I[:, 2:3], r="P15c", w="ROT")
+    v(V.tensor_scalar, T.S5[:], T.SI[:], 5, None, A.mult, r="SI", w="S5")
+    v(V.tensor_scalar, T.BC[:], T.THF[:], -1, None, A.mult, r="THF", w="BC")
+
+    def consts_late():
+        v(V.memset, T.ONEF[:], 1.0, w="ONEF")
+        v(V.memset, T.NEG[:], -128.0, w="NEG")
+        v(V.memset, T.X[:, 4096:8192], 0.0, w="XD")
+        v(V.memset, T.SH[:, 768:1024], 0.0, w="SH3")
+        v(V.memset, T.SH[:, 1536:1792], 0.0, w="SH6")
+
+    shk = "SH3 SH6 SHf SHg " + " ".join("SA%d SB%d" % (h, h) for h in (8, 5, 3, 2, 1, 0))
+
+    def thr(ncol, nkey):
+        v(V.tensor_scalar, T.N1[:], ncol, 1, 16, A.add, A.min, r=nkey, w="N1")
+        for h in HS:
+            e = BASE[h] + h - 1
+            v(V.tensor_scalar, T.THR[:, e:320:20], T.N1[:], 0.5 - 2 * h, 0.0, A.add, A.min, r="N1 THR", w="THR%d" % e)
+    thk = "THR THR0 " + " ".join("THR%d" % (BASE[h] + h - 1) for h in HS)
+
+    def bound():
+        act(T.RB[:], T.DB[:], scale=T.BC[:], r="DB BC", w="RB")
+
+    def build_sh(t):
+        for h in (8, 5, 3, 2, 1, 0):
+            c, d = 256 * SLOT[h], 17 - h
+            dma("sh", T.SH[d:128, c:c + 256], T.W2R[0:128 - d, 256 * t:256 * t + 256], r="W2R%d" % t, w="SA%d" % h)
+            dma("sh", T.SH[0:d, c:c + 256], T.W2R[128 - d:128, 256 * t:256 * t + 256], r="W2R%d" % t, w="SB%d" % h)
+        dma("sh2", T.SH[17:128:16, 1280:1536], T.LFR[0:112:16, 256 * t:256 * t + 256], r="LFR%d SA0 SB0" % t, w="SHf")
+        dma("sh2", T.SH[1:2, 1280:1536], T.LFR[112:113, 256 * t:256 * t + 256], r="LFR%d SA0 SB0" % t, w="SHg")
+
+    def idx(h, j):
+        return PAIRS.index((h, j))
+
+    def pd(hf, lo, hi):
+        return (T.PD0 if hf == 0 else T.PD1)[:, lo:hi]
+
+    def place(hf, h, j):
+        return (T.PD0 if hf == 0 else T.PD1)[:, BASE[h] + j:160:20]
+
+    def bulk(t):
+        PGK = "PG0 PG1 PG2 PG3"
+        act(T.GL[:, 0:1024], T.X[:, 0:4096].indirect(T.LH[:, 0:64]), r="X LH", w="GLa")
+        v(V.tensor_copy, T.GL[:, 1024:2048], T.X[:, 0:4096].indirect(T.LH[:, 64:128]), r="X LH", w="GLb")
+        act(T.GH[:, 0:1024], T.X[:, 0:4096].indirect(T.LH[:, 128:192]), r="X LH", w="GHa")
+        act(T.GH[:, 1024:2048], T.X[:, 0:4096].indirect(T.LH[:, 192:256]), r="X LH", w="GHb")
+        for b_ in range(4):
+            mm(T.PG[:, 512 * b_:512 * b_ + 512], T.IDB[:], T.GL[:, 512 * b_:512 * b_ + 512], r="IDB GL" + "ab"[b_ // 2], w="pg", b="PG%d" % b_)
+        thr(T.N0[:], "N0")
+        if t == 0:
+            consts_late()
+        for hf in range(2):
+            mm(pd(hf, 0, 160), T.ONE[:], T.RB[:], True, False, r="ONE RB", w="pd%d" % hf, b="PD%d" % hf)
+
+        def low(hf, j):
+            k_ = {(0, 0): 0, (0, 1): 1, (0, 2): 2, (1, 0): 3}.get((hf, j))
+            gl = T.GL[:, 1024 * hf + j:1024 * hf + 1024:8]
+            key = "GL%s%s" % ("ab"[hf], " GL0" if j == 0 else "")
+            if k_ is not None:
+                mm(pd(hf, 0, 160), gl, T.CP[:, 160 * k_:160 * k_ + 160], False, False, r=key + cpk, w="pd%d" % hf, b="PD%d" % hf)
+                return
+            for h in HS:
+                if h > j and not (h == 8 and hf == 1):
+                    mm(place(hf, h, j), gl, T.KN[:], False, False, r=key + " KN", w="pd%d" % hf, b="PD%d" % hf)
+
+        def high(hf, rr):
+            for h in HS:
+                j = rr - h
+                if 0 <= j < h and not (h == 8 and hf == 1):
+                    src, key = (T.GL, "GL") if rr < 8 else (T.GH, "GH")
+                    o = 1024 * hf + rr % 8
+                    mm(place(hf, h, j), src[:, o:1024 * hf + 1024:8], T.KN[:], False, False, r=key + "ab"[hf] + " KN", w="pd%d" % hf, b="PD%d" % hf)
+
+        def add(hf, h, j, last=False):
+            o = place(hf, h, j)
+            if h == 8:
+                mm(o, T.D8[:, 1024 * hf + j:1024 * hf + 1024:8], T.K2[:] if hf == 0 else T.KB[:], False, last,
+                   r=("K2 D8a D8b" + (" D8j" if j == 0 else "")) if hf == 0 else "KB D8c D8d", w="pd%d" % hf, b="PD%d" % hf)
+            else:
+                c = 256 * idx(h, j) + 128 * hf
+                mm(o, T.DL[:, c:c + 128], T.K2[:], False, last, r="K2 DL%d%d" % (h, j), w="pd%d" % hf, b="PD%d" % hf)
+
+        def pair(h, j):
+            c = 256 * idx(h, j)
+            if j == 0:
+                i0, i1, key = T.PG[:, h:2048:8], T.GL[:, 0:2048:8], "GL0"
+            elif j + h < 8:
+                i0, i1, key = T.PG[:, j:2048:8], T.GL[:, j + h:2048:8], "GLa GLb"
+            else:
+                i0, i1, key = T.PG[:, j:2048:8], T.GH[:, j + h - 8:2048:8], "GHa GHb"
+            v(V.tensor_tensor, T.DL[:, c:c + 256], i0, i1, A.max, r="pg " + key, w="DL%d%d" % (h, j), b=PGK)
+
+        for hf in range(2):
+            for rr in range(1, 8):
+                low(hf, rr)
+                high(hf, rr)
+        early = ((2, 1), (3, 1), (3, 2), (5, 1), (5, 2))
+        for h, j in early:
+            pair(h, j)
+            for hf in range(2):
+                add(hf, h, j)
+        for rr in range(8, 16):
+            high(0, rr)
+        for b_ in range(2):
+            v(V.tensor_tensor, T.D8[:, 512 * b_:512 * b_ + 512], T.PG[:, 512 * b_:512 * b_ + 512], T.GH[:, 512 * b_:512 * b_ + 512], A.max, r="pg GHa", w="D8" + "ab"[b_], b="PG%d" % b_)
+        for j in range(1, 8):
+            add(0, 8, j)
+        high(1, 8)
+        high(1, 9)
+        if t > 0:
+            v(V.tensor_copy, T.LLU[:], T.MNR[:, 32 * (t - 1) + 16:32 * t], r="MNR%d" % (t - 1), w="LLU")
+            v(V.tensor_scalar, T.S5[:], T.MNR[:, 32 * (t - 1):32 * (t - 1) + 16], 5, None, A.mult, r="MNR%d" % (t - 1), w="S5")
+        act(T.GL[:, 0:2048:8], T.X[:, 0:4096].indirect(T.LLU[:]), r="X LLU", w="GL0 GLa GLb")
+        for h, j in ((5, 3), (5, 4)):
+            pair(h, j)
+            for hf in range(2):
+                add(hf, h, j)
+        for b_, B, bk in ((2, T.B4, "B4"), (3, T.B5, "B5")):
+            mm(B[:], T.IDB[:], T.GL[:, 512 * b_:512 * b_ + 512], True, False, r="IDB GL0 GLb", w="pB", b=bk)
+            mm(B[:], T.NIB[:], T.GH[:, 512 * b_:512 * b_ + 512], False, True, r="NIB GHb", w="pB" + bk, b=bk)
+            act(T.D8[:, 512 * b_:512 * b_ + 512], B[:], F.Abs, r="pB" + bk, w="D8" + "abcd"[b_], b=bk)
+        for hf in range(2):
+            low(hf, 0)
+        for h in (5, 3, 2, 1):
+            pair(h, 0)
+            for hf in range(2):
+                add(hf, h, 0)
+        v(V.tensor_tensor, T.D8[:, 0:1024:8], T.GL[:, 0:1024:8], T.GH[:, 0:1024:8], A.max, r="GL0 GHa D8a D8b", w="D8j")
+        add(0, 8, 0, True)
+        for j in range(8):
+            add(1, 8, j, j == 7)
+        v(V.tensor_tensor_scan, T.ZC[:], T.ZR[:], T.GL[:], 0.0, A.mult, A.max, r="ZR GLa GLb GL0", w="ZC")
+        act(T.ZC[:, 5:2048:8], T.GL[:, 0:2048:8], r="GL0 ZC", w="ZC5")
+
+    def decode(t):
+        last = t == TV - 1
+        rs = 16 if last else 0
+        m1 = 288 * t
+        for hf in range(2):
+            B, bk = (T.B4, "B4") if hf == 0 else (T.B5, "B5")
+            c = 160 * hf
+            v(V.tensor_tensor_scan, B[:, 0:160], T.D0[:], pd(hf, 0, 160), 0.0, A.mult, A.max, r="pd%d %s" % (hf, d0k), w="s1%d" % hf, b="PD%d %s" % (hf, bk))
+            v(V.tensor_tensor, T.E[:, c:c + 160], B[:, 0:160], T.THR[:, c:c + 160], A.is_gt, r="s1%d %s" % (hf, thk), w="E%d" % hf, b=bk)
+            v(V.tensor_tensor_scan, T.SC2[:, c:c + 160], T.E[:, c:c + 160], T.C2[:], 0.0, A.mult, A.add, r="E%d %s" % (hf, c2k), w="SC%d" % hf)
+        v(V.tensor_tensor, T.EK[:], T.SC2[:].indirect(T.LK9[:]), T.ME[:], A.mult, r="SC0 SC1 LK9 ME", w="EK")
+        mm(T.PG[:, 0:16], T.IDB[:], T.B8[:], True, False, r="IDB B8", w="p1", b="PG0")
+        for hf in range(2):
+            mm(T.PG[:, 8 * hf:8 * hf + 8], T.EK[:, 144 * hf + 16:144 * hf + 144], T.KB[:], False, hf == 1, r="EK KB", w="p1", b="PG0")
+        for hf in range(2):
+            mm(T.PG[:, 512 + 8 * hf:520 + 8 * hf], T.EK[:, 144 * hf + rs:144 * hf + rs + 128], T.K256[:], r="EK K256", w="p2", b="PG1")
+        kap = T.SC2[:, 19:320:20]
+        v(V.tensor_scalar, T.NH[:], kap, 5, None, A.is_equal, r="SC0 SC1", w="NH")
+        v(V.tensor_copy, T.L1[:], T.PG[:, 0:16], r="p1", w="L1", b="PG0")
+        v(V.tensor_copy, T.M1S[:, m1:m1 + 128], T.ZC[:].indirect(T.L1[:, 0:8]), r="ZC ZC5 L1", w="Za")
+        act(T.M1S[:, m1 + 128:m1 + 256], T.ZC[:].indirect(T.L1[:, 8:16]), r="ZC ZC5 L1", w="Zb")
+        act(T.M1S[:, m1 + 256:m1 + 272], T.PG[:, 512:528], r="p2", w="Zc", b="PG1")
+        for hf in range(2):
+            mm(T.PG[:, 1024 + 8 * hf:1032 + 8 * hf], T.M1S[:, m1 + 128 * hf:m1 + 128 * hf + 128], T.WTB[:], r="Z%s WTB" % "ab"[hf], w="pt", b="PG2")
+        mm(T.PG[:, 1536:1552], T.IDB[:], T.B16[:], True, False, r="IDB B16", w="p3", b="PG3")
+        v(V.tensor_scalar, T.H1[:], T.NH[:], -6, 1, A.mult, A.add, r="NH", w="H1")
+        v(V.tensor_tensor, T.S5[:], T.S5[:], T.NH[:], A.mult, r="S5 NH", w="S5")
+        v(V.tensor_tensor, T.H[:], T.H1[:], kap, A.add, r="H1 SC0 SC1", w="H")
+        v(V.tensor_scalar, T.DU[:], T.NH[:], 4096, None, A.mult, r="NH", w="DU")
+        v(V.tensor_tensor, T.AD[:], T.S5[:], T.H[:], A.add, r="S5 H", w="AD")
+        v(V.tensor_tensor, T.NP[:], T.N1[:], T.H[:], A.subtract, r="N1 H", w="NP")
+        if last:
+            v(V.tensor_copy, T.M1S[:, m1 + 272:m1 + 288], T.NP[:], r="NP", w="Zd")
+        else:
+            v(V.tensor_copy, T.M1S[:, m1 + 272:m1 + 288], T.NP[:].indirect(T.ROT[:, 0:1]), r="NP ROT", w="Zd")
+        v(V.tensor_tensor, T.SUM[:], T.PG[:, 1024:1040], T.AD[:], A.add, r="pt AD", w="SUM", b="PG2")
+        v(V.tensor_scalar, T.V15[:], T.SUM[:], 15, None, A.bitwise_and, r="SUM", w="V15")
+        v(V.tensor_tensor, T.VV[:], T.V15[:], T.DU[:], A.max, r="V15 DU", w="VV")
+        v(V.tensor_tensor, T.EV[:], T.VV[:].indirect(T.LU[:]), T.ME[:, 0:256], A.mult, r="VV LU ME", w="EV")
+        for hf in range(2):
+            mm(T.PG[:, 1536 + 8 * hf:1544 + 8 * hf], T.EV[:, 128 * hf:128 * hf + 128], T.KB[:], False, hf == 1, r="EV KB", w="p3", b="PG3")
+        v(V.tensor_copy, T.MLS[:, 16 * t:16 * t + 16], T.PG[:, 1536:1552], r="p3", w="MLS", b="PG3")
+        send("M1%d" % t, nxt, T.M1R[:, m1:m1 + 288], T.M1S[:, m1:m1 + 288], r="Za Zb Zc Zd")
+        send("ML%d" % t, nxt, T.MLR[:, 16 * t:16 * t + 16], T.MLS[:, 16 * t:16 * t + 16], r="MLS")
+        v(V.tensor_scalar, T.SI[:], T.SUM[:], 4095, None, A.bitwise_and, r="SUM", w="SI")
+        return last
+
+    def xupdate(t, a=0, b=16, tag=""):
+        cols = T.MLR[:, 16 * t + a:16 * t + b]
+        n0, n1 = 16 * a, 16 * b
+        v(V.tensor_tensor, T.XT[:, n0:n1], T.X[:].indirect(cols), T.M1R[:, 288 * t + n0:288 * t + n1], A.add, r="X XD MLR%d M1R%d" % (t, t), w="XT")
+        v(V.tensor_scalar, T.XU[:, n0:n1], T.XT[:, n0:n1], 0.5, 127.75, A.mult, A.add, r="XT", w="XU")
+        v(V.tensor_tensor, T.X[:].indirect(cols), T.XU[:, n0:n1], T.NEG[:, n0:n1], A.add, r="XU NEG MLR%d" % t, w="X XD")
+
+    for t in range(TV):
+        if t < TV - 1:
+            send("W2%d" % t, nxt, T.W2R[:, 256 * t:256 * t + 256], T.W2[:, 256 * t:256 * t + 256], r="W2%d" % t)
+            build_sh(t)
+        else:
+            for h in (8, 5, 3, 2, 1, 0):
+                c = 256 * SLOT[h]
+                dma("sh", T.SH[0:128 - h, c:c + 256], T.W2[h:128, 1024:1280], r="W24", w="SA%d SB%d" % (h, h))
+            dma("sh2", T.SH[0:128:16, 1280:1536], T.LFR[0:128:16, 1024:1280], r="LFR4 SA0 SB0", w="SHf SHg")
+        if t == 0:
+            bound()
+        bulk(t)
+        decode(t)
+        if t == TV - 1:
+            break
+        u = t + 1
+        m1 = 288 * t
+        push1(T.NP[:], "NP")
+        v(V.tensor_copy, T.MNS[:, 32 * t:32 * t + 16], T.SI[:].indirect(T.ROT[:, 0:1]), r="SI ROT", w="MNa")
+        v(V.tensor_tensor, T.KBI[:], T.M1R[:, m1 + 256:m1 + 272], T.BI[:], A.add, r="M1R%d BI" % t, w="KBI")
+        v(V.tensor_copy, T.L2[:], T.KBI[:], r="KBI", w="L2")
+        act(T.W2[:, 256 * u:256 * u + 256], T.SH[:].indirect(T.L2[:]), r="L2 " + shk, w="W2%d" % u)
+        push2(0)
+        rearr(u)
+        push2b("LSN")
+        v(V.tensor_reduce, T.NS[:], T.NH[:], AxisListType.X, A.add, r="NH", w="NS")
+        mm(T.B5[:, 0:1], T.ONEF[:], T.NS[:], r="ONEF NS", w="pA", b="B5")
+        v(V.tensor_scalar, T.AI[:], T.B5[:, 0:1], -1, 2048, A.mult, A.add, r="pA", w="AI", b="B5")
+        v(V.tensor_scalar, T.AJ[:], T.AI[:], 15, None, A.bitwise_and, r="AI", w="AJ")
+        v(V.tensor_scalar, T.BC[:], T.AJ[:], T.THF[:], -1, A.add, A.mult, r="AJ THF", w="BC")
+        bound()
+        v(V.tensor_copy, T.N0[:], T.M1R[:, m1 + 272:m1 + 288], r="M1R%d" % t, w="N0")
+        push3(u)
+        xupdate(t)
+        lists()
+        push4()
+        act(T.MNS[:, 32 * t + 16:32 * t + 32], T.B5[:, 0:16], r="pL", w="MNb", b="B5")
+        send("MN%d" % t, nxt, T.MNR[:, 32 * t:32 * t + 32], T.MNS[:, 32 * t:32 * t + 32], r="MNa MNb")
+        send("LF%d" % u, nx2 if u < 4 else nxt, T.LFR[:, 256 * u:256 * u + 256], T.LF[:, 256 * u:256 * u + 256], r="LF%d" % u)
+
+    v(V.tensor_copy, T.SF[:], T.SI[:], r="SI", w="SF")
+    v(V.tensor_tensor, T.KBI[:], T.M1S[:, 4 * 288 + 256:4 * 288 + 272], T.BI[:], A.add, r="Zc BI", w="KBI")
+    v(V.tensor_copy, T.L2[:], T.KBI[:], r="KBI", w="L2")
+    v(V.tensor_copy, T.RS[:], T.NP[:].indirect(T.LS9[:]), r="NP LS9", w="RS")
+    for hf in range(2):
+        mm(T.PG[:, 512 + 128 * hf:640 + 128 * hf], T.RS[:, 144 * hf + 16:144 * hf + 144], T.IDB[:], r="RS IDB", w="pR", b="PG1")
+    for hf in range(2):
+        mm(T.PG[0:8, 128 * hf:128 * hf + 128], T.NP[:, 8 * hf:8 * hf + 8], T.IDF[:], r="NP IDF", w="pN", b="PG0")
+    for hf in range(2):
+        mm(T.PG[0:8, 1024 + 128 * hf:1152 + 128 * hf], T.SF[:, 8 * hf:8 * hf + 8], T.IDF[:], r="SF IDF", w="pS", b="PG2")
+    v(V.tensor_scalar, T.MK[:], T.PG[:, 512:768], T.P15[:], None, A.is_gt, r="pR P15", w="MK", b="PG1")
+    v(V.tensor_tensor, T.YW[:], T.SH[:].indirect(T.L2[:]), T.MK[:], A.mult, r="L2 MK " + shk, w="YW")
+    dma("oyw", T.yw[:], T.YW[:], r="YW")
+    xupdate(4)
+    dma("oyx", T.yx[:], T.X[:, 0:4096], r="X")
+    act(T.YN[:], T.PG[0:8, 0:256], r="pN", w="YN", b="PG0")
+    act(T.YS[:], T.PG[0:8, 1024:1280], r="pS", w="YS", b="PG2")
+    dma("oyn", T.yn[:], T.YN[:], r="YN")
+    dma("oyn", T.ys[:], T.YS[:], r="YS")
+    for sem, n in tot.items():
+        if known["g"].get(sem, 0) < n:
+            g.wait_ge(T.sem[sem], n)

@@ -21,7 +21,7 @@ SCRATCH = {
     "RA": ("sbuf", [128, 512], "float32"), "ME": ("sbuf", [128, 288], "float32"),
     "KB": ("sbuf", [128, 8], "bfloat16"), "KF": ("sbuf", [128, 8], "float32"), "K256": ("sbuf", [128, 8], "bfloat16"),
     "K2": ("sbuf", [128, 8], "bfloat16"), "KN": ("sbuf", [128, 8], "bfloat16"), "WTB": ("sbuf", [128, 8], "bfloat16"),
-    "CP": ("sbuf", [128, 640], "bfloat16"), "DB": ("sbuf", [128, 160], "bfloat16"), "RB": ("sbuf", [128, 160], "bfloat16"),
+    "CP": ("sbuf", [128, 1280], "bfloat16"), "DB": ("sbuf", [128, 160], "bfloat16"), "RB": ("sbuf", [128, 160], "bfloat16"),
     "D0": ("sbuf", [128, 160], "bfloat16"), "C2": ("sbuf", [128, 160], "bfloat16"), "THR": ("sbuf", [128, 320], "float32"),
     "E": ("sbuf", [128, 320], "bfloat16"), "SC2": ("sbuf", [128, 320], "bfloat16"),
     "EK": ("sbuf", [128, 288], "bfloat16"), "EC": ("sbuf", [128, 288], "float32"), "RS": ("sbuf", [128, 288], "bfloat16"),
@@ -152,9 +152,9 @@ def rank_program(g, core, T, topo):
     v(V.memset, T.THI[:], 0, w="THI")
     dma("small", T.SDI[:], T.sd[:], w="SDI")
     dma("small", T.NLI[:], T.nl[:], w="NLI")
-    dma("ls", T.LS[:], T.ls[:], w="LS")
     dma("wd", T.WI[1:128, :], T.wd[0:127, :], w="WIa")
     dma("wd", T.WI[0:1, :], T.wd[0:1, :], w="WIb")
+    dma("ls", T.LS[:], T.ls[:], w="LS")
     dma("sm2", T.THI[0:128:16, :], T.th[:], w="THI")
     dma("sm2", T.WTI[:], T.wt[:], w="WTI")
     dma("x", T.X[:, 0:4096], T.x[:], w="X")
@@ -172,13 +172,36 @@ def rank_program(g, core, T, topo):
     iota(T.IU[:], [[1, 16]], 0, 0, "IU")
     iota(T.IK[:], [[16, 16]], 0, 0, "IK")
     iota(T.I20[:], [[-16, 8], [0, 20]], 0, 1, "I20")
+    v(V.memset, T.ZR[:], 1.0, w="ZR")
+    act(T.CP[:], T.ZR[:, 0:1280], scale=0.0, r="ZR", w="CP")
+    for c in (4096, 6144):
+        act(T.X[:, c:c + 2048], T.ZR[:], scale=0.0, r="ZR", w="XD")
+    d0k = "D0 " + " ".join("D0%d" % q_ for q_ in (0, 1, 9, 14, 17, 19))
+    c2k = "C2 C20 C28 C213 C216 C218"
+
+    def consts_scan():
+        v(V.memset, T.D0[:], 1.0, w="D0")
+        v(V.memset, T.C2[:], 0.0, w="C2")
+        for q_ in (0, 1, 9, 14, 17, 19):
+            v(V.memset, T.D0[:, q_:160:20], 0.0, r="D0", w="D0%d" % q_)
+        for q_, c in ((0, -2.0), (8, 3.0), (13, 2.0), (16, 1.0), (18, 1.0)):
+            v(V.memset, T.C2[:, q_:160:20], c, r="C2", w="C2%d" % q_)
+
     v(V.tensor_scalar, T.IDF[:], T.II[:], 0, None, A.is_equal, r="II", w="IDF")
+    v(V.tensor_scalar, T.P15I[:, 1:2], T.IP[:, 0:1], 3, 1, A.arith_shift_right, A.bitwise_and, r="IP", w="P15b")
+    v(V.tensor_copy, T.PB[:, 1:2], T.P15I[:, 1:2], r="P15b", w="PB1")
+    v(V.tensor_scalar, T.PB[:, 0:1], T.P15I[:, 1:2], -1, 1, A.mult, A.add, r="P15b", w="PB0")
+    for b_ in range(2):
+        for w_ in range(2):
+            c = 128 * (2 * b_ + w_)
+            v(V.tensor_scalar, T.RA[:, c:c + 128], T.II[:], 8 * (b_ - w_), T.PB[:, b_:b_ + 1], A.is_equal, A.mult, r="II PB%d" % b_, w="RA%d%d" % (b_, w_))
     v(V.tensor_copy, T.SDF[:], T.SDI[:], r="SDI", w="SDF")
     v(V.tensor_copy, T.NLF[:], T.NLI[:], r="NLI", w="NLF")
     for hf in range(2):
         mm(T.B4[:, 8 * hf:8 * hf + 8], T.SDF[:, 128 * hf:128 * hf + 128], T.IDF[0:8, 0:8], r="SDF IDF", w="B4sd", b="B4")
     for hf in range(2):
         mm(T.B4[:, 16 + 8 * hf:24 + 8 * hf], T.NLF[:, 128 * hf:128 * hf + 128], T.IDF[0:8, 0:8], r="NLF IDF", w="B4sd", b="B4")
+    v(V.memset, T.ROW0[:], 0.0, w="ROW0")
     v(V.tensor_scalar, T.IG[:], T.IG[:], 4, None, A.arith_shift_right, r="IG", w="IG")
     v(V.tensor_scalar, T.KB[:], T.IG[:], 0, None, A.is_equal, r="IG", w="KB")
     v(V.tensor_scalar, T.KF[:], T.IG[:], 0, None, A.is_equal, r="IG", w="KF")
@@ -193,10 +216,13 @@ def rank_program(g, core, T, topo):
     v(V.tensor_copy, T.P15[:], T.P15I[:, 0:1], r="P15I", w="P15")
     v(V.tensor_copy, T.IDB[:], T.IDF[:], r="IDF", w="IDB")
 
-    def push1(ncol, nkey):
-        v(V.tensor_tensor, T.T1[:], T.SI[:], T.SI[:], A.mult, r="SI", w="T1")
-        v(V.tensor_scalar, T.U[:], ncol, 77, None, A.mult, r=nkey, w="U")
+    def push1(ncol, nkey, first=None):
+        if not first:
+            v(V.tensor_tensor, T.T1[:], T.SI[:], T.SI[:], A.mult, r="SI", w="T1")
+            v(V.tensor_scalar, T.U[:], ncol, 77, None, A.mult, r=nkey, w="U")
         v(V.tensor_scalar, T.S15[:], T.SI[:], 15, None, A.bitwise_and, r="SI", w="S15")
+        if first:
+            first()
         v(V.tensor_scalar, T.T2[:], T.T1[:], 5, None, A.arith_shift_right, r="T1", w="T2")
         v(V.tensor_tensor, T.U[:], T.U[:], T.SI[:], A.add, r="U SI", w="U")
         v(V.tensor_tensor, T.T1[:], T.T2[:], T.U[:], A.add, r="T2 U", w="T1")
@@ -214,94 +240,73 @@ def rank_program(g, core, T, topo):
         v(V.tensor_copy, T.CL[:], T.PG[:, 0:16], r="pC", w="CL", b="PG0")
         v(V.tensor_scalar, T.MK[:], T.PG[:, 512:768], T.P15[:], None, A.is_equal, r="pR P15", w="MK", b="PG1")
         v(V.tensor_tensor, T.MM[:], T[ls][:].indirect(T.CL[:]), T.MK[:], A.mult, r=ls + " CL MK", w="MM")
+
+    def push2w():
         for hf in range(2):
             mm(T.PG[:, 1024 + 8 * hf:1032 + 8 * hf], T.MM[:, 128 * hf:128 * hf + 128], T.KF[:], r="MM KF", w="pW", b="PG2")
-        mm(T.PG[:, 1536:1792], T.ROW0[:], T.MM[:], r="MM ROW0", w="pF", b="PG3")
 
-    def push3(t):
+    def push2f():
+        mm(T.B5[:, 256:512], T.ROW0[:], T.MM[:], r="MM ROW0", w="pF", b="B5")
+
+    def push3():
         v(V.tensor_copy, T.LW[:], T.PG[:, 1024:1040], r="pW", w="LW", b="PG2")
-        act(T.LF[:, 256 * t:256 * t + 256], T.PG[:, 1536:1792], r="pF", w="LF%d" % t, b="PG3")
+
+    def push3f(t):
+        act(T.LF[:, 256 * t:256 * t + 256], T.B5[:, 256:512], r="pF", w="LF%d" % t, b="B5")
 
     def push4():
         v(V.tensor_tensor, T.EL[:], T.LW[:].indirect(T.LU[:]), T.ME[:, 0:256], A.mult, r="LW LU ME", w="EL")
         for hf in range(2):
             mm(T.B5[:, 8 * hf:8 * hf + 8], T.EL[:, 128 * hf:128 * hf + 128], T.KF[:], r="EL KF", w="pL", b="B5")
 
+    v(V.tensor_copy, T.W2[:, 0:256], T.WI[:], r="WIa WIb", w="W20")
     push1(T.N0[:], "N0")
-    v(V.memset, T.ROW0[:], 0.0, w="ROW0")
-    v(V.tensor_copy, T.ROW0[:, 0:128:16], T.KF[:], r="KF", w="ROW0")
-    push2(16)
-    push2b("LS")
-    v(V.tensor_scalar, T.P15I[:, 1:2], T.IP[:, 0:1], 3, 1, A.arith_shift_right, A.bitwise_and, r="IP", w="P15b")
-    v(V.tensor_copy, T.PB[:, 1:2], T.P15I[:, 1:2], r="P15b", w="PB1")
-    v(V.tensor_scalar, T.PB[:, 0:1], T.P15I[:, 1:2], -1, 1, A.mult, A.add, r="P15b", w="PB0")
-    for b_ in range(2):
+
+    def rearr(t, b_):
+        w2 = 256 * t
+        out, bk = (T.B4[:, 128:256], "B4") if b_ == 0 else (T.PG[:, 1792:1920], "PG3")
         for w_ in range(2):
             c = 128 * (2 * b_ + w_)
-            v(V.tensor_scalar, T.RA[:, c:c + 128], T.II[:], 8 * (b_ - w_), T.PB[:, b_:b_ + 1], A.is_equal, A.mult, r="II PB%d" % b_, w="RA%d%d" % (b_, w_))
-    v(V.tensor_copy, T.W2[:, 0:256], T.WI[:], r="WIa WIb", w="W20")
-    push3(0)
+            mm(out, T.RA[:, c:c + 128], T.W2[:, w2 + w_:w2 + 256:2], w_ == 0, w_ == 1, r="W2%d RA%d%d" % (t, b_, w_), w="pH%d" % b_, b=bk)
+
+    def lists(b_):
+        src, bk = (T.B4[:, 128:256], "B4") if b_ == 0 else (T.PG[:, 1792:1920], "PG3")
+        v(V.tensor_copy, T.LH[:, 128 * b_:128 * b_ + 128], src, r="pH%d" % b_, w="LH%d" % b_, b=bk)
+
+    push2(16)
+    rearr(0, 0)
+    rearr(0, 1)
+    lists(0)
+    lists(1)
+    act(T.KN[:], T.KB[:], scale=-1.0, r="KB", w="KN")
+    act(T.K2[:], T.KB[:], scale=2.0, r="KB", w="K2")
+    act(T.NIB[:], T.IDB[:], scale=-1.0, r="IDB", w="NIB")
+    act(T.ROW0[:, 0:128:16], T.KF[:], r="KF", w="ROW0")
+    cpk = [["CP"] * 4, ["CP"] * 4]
+    for rr in (1, 2, 3, 0):
+        for hf in range(2):
+            for h in HS[hf:]:
+                for j in (rr, rr - h):
+                    if 0 <= j < h:
+                        key, c = "CP%d%d%d" % (hf, rr, h), 160 * (4 * hf + rr) + BASE[h] + j
+                        act(T.CP[:, c:160 * (4 * hf + rr) + 160:20], T.KN[:], r="KN CP", w=key)
+                        cpk[hf][rr] += " " + key
+    act(T.SH[:, 768:1024], T.W2[:, 0:256], scale=0.0, r="W20", w="SH3")
+    act(T.SH[:, 1536:1792], T.W2[:, 0:256], scale=0.0, r="W20", w="SH6")
+    act(T.ONEF[:], T.IDF[:], F.Identity, scale=0.0, bias=1.0, r="IDF", w="ONEF")
+    act(T.NEG[:], T.W2[:, 0:256], F.Identity, scale=0.0, bias=-128.0, r="W20", w="NEG")
+    push2b("LS")
+    push2w()
+    push3()
     push4()
     v(V.tensor_copy, T.LLU[:], T.B5[:, 0:16], r="pL", w="LLU", b="B5")
-    send("LF0", nxt, T.LFR[:, 0:256], T.LF[:, 0:256], r="LF0")
+    push2f()
+    push3f(0)
     send("LS", prv, T.LSN[:], T.LS[:], r="LS")
-
-    def rearr(t):
-        w2 = 256 * t
-        for b_ in range(2):
-            for w_ in range(2):
-                c = 128 * (2 * b_ + w_)
-                mm(T.B4[:, 128 * b_:128 * b_ + 128], T.RA[:, c:c + 128], T.W2[:, w2 + w_:w2 + 256:2], w_ == 0, w_ == 1, r="W2%d RA%d%d" % (t, b_, w_), w="pH", b="B4")
-
-    def lists():
-        v(V.tensor_copy, T.LH[:], T.B4[:, 0:256], r="pH", w="LH", b="B4")
-
-    rearr(0)
-    lists()
-    v(V.tensor_copy, T.WTF[:], T.WTI[:], r="WTI", w="WTF")
+    send("LF0", nxt, T.LFR[:, 0:256], T.LF[:, 0:256], r="LF0")
     v(V.tensor_copy, T.THF[:], T.THI[:], r="THI", w="THF")
-    v(V.tensor_scalar, T.WTB[:], T.KB[:], T.WTF[:], None, A.mult, r="KB WTF", w="WTB")
-    v(V.tensor_scalar, T.K2[:], T.KB[:], 2, None, A.mult, r="KB", w="K2")
-    v(V.tensor_scalar, T.KN[:], T.KB[:], -1, None, A.mult, r="KB", w="KN")
-    v(V.tensor_scalar, T.K256[:], T.KB[:], 256, None, A.mult, r="KB", w="K256")
     v(V.tensor_scalar, T.DB[:], T.I20[:], 0, None, A.is_equal, r="I20", w="DB")
-    v(V.memset, T.CP[:], 0.0, w="CP")
-    for h in HS:
-        for k_, j in ((0, 0), (1, 1), (2, 2), (3, 0)):
-            if h > j and not (k_ == 3 and h == 8):
-                v(V.tensor_copy, T.CP[:, 160 * k_ + BASE[h] + j:160 * k_ + 160:20], T.KN[:], r="KN CP", w="CP%d%d" % (k_, h))
-    cpk = " CP " + " ".join("CP%d%d" % (k_, h) for k_ in range(4) for h in HS)
-    v(V.memset, T.ONE[:], 1.0, w="ONE")
-    v(V.tensor_scalar, T.NIB[:], T.IDB[:], -1, None, A.mult, r="IDB", w="NIB")
-    v(V.memset, T.ZR[:], 1.0, w="ZR")
-    v(V.memset, T.ZR[:, 0:2048:8], 0.0, w="ZR")
-    v(V.memset, T.D0[:], 1.0, w="D0")
-    for q_ in (0, 1, 9, 14, 17, 19):
-        v(V.memset, T.D0[:, q_:160:20], 0.0, r="D0", w="D0%d" % q_)
-    d0k = "D0 " + " ".join("D0%d" % q_ for q_ in (0, 1, 9, 14, 17, 19))
-    v(V.memset, T.C2[:], 0.0, w="C2")
-    for q_, c in ((0, -2.0), (8, 3.0), (13, 2.0), (16, 1.0), (18, 1.0)):
-        v(V.memset, T.C2[:, q_:160:20], c, r="C2", w="C2%d" % q_)
-    c2k = "C2 C20 C28 C213 C216 C218"
-    v(V.memset, T.THR[:], -1.0, w="THR")
-    v(V.memset, T.THR[:, 0:320:20], 1000.0, r="THR", w="THR0")
-    v(V.tensor_scalar, T.BI[:], T.IK[:], T.P15[:], None, A.add, r="IK P15", w="BI")
-    v(V.tensor_scalar, T.B8[:], T.BI[:], 8, None, A.mult, r="BI", w="B8")
-    v(V.tensor_scalar, T.B16[:], T.BI[:], 16, None, A.mult, r="BI", w="B16")
-    v(V.tensor_scalar, T.P15I[:, 2:3], T.P15I[:, 0:1], 8, None, A.bitwise_and, r="P15I", w="P15c")
-    v(V.tensor_scalar, T.P15I[:, 3:4], T.P15I[:, 0:1], -1, None, A.add, r="P15I", w="P15d")
-    v(V.tensor_scalar, T.P15I[:, 3:4], T.P15I[:, 3:4], 7, None, A.bitwise_and, r="P15d", w="P15d")
-    v(V.tensor_tensor, T.P15I[:, 2:3], T.P15I[:, 2:3], T.P15I[:, 3:4], A.add, r="P15c P15d", w="P15c")
-    v(V.tensor_copy, T.ROT[:, 0:1], T.P15I[:, 2:3], r="P15c", w="ROT")
-    v(V.tensor_scalar, T.S5[:], T.SI[:], 5, None, A.mult, r="SI", w="S5")
     v(V.tensor_scalar, T.BC[:], T.THF[:], -1, None, A.mult, r="THF", w="BC")
-
-    def consts_late():
-        v(V.memset, T.ONEF[:], 1.0, w="ONEF")
-        v(V.memset, T.NEG[:], -128.0, w="NEG")
-        v(V.memset, T.X[:, 4096:8192], 0.0, w="XD")
-        v(V.memset, T.SH[:, 768:1024], 0.0, w="SH3")
-        v(V.memset, T.SH[:, 1536:1792], 0.0, w="SH6")
 
     shk = "SH3 SH6 SHf SHg " + " ".join("SA%d SB%d" % (h, h) for h in (8, 5, 3, 2, 1, 0))
 
@@ -313,7 +318,7 @@ def rank_program(g, core, T, topo):
     thk = "THR THR0 " + " ".join("THR%d" % (BASE[h] + h - 1) for h in HS)
 
     def bound():
-        act(T.RB[:], T.DB[:], scale=T.BC[:], r="DB BC", w="RB")
+        v(V.tensor_scalar, T.RB[:], T.DB[:], T.BC[:], None, A.mult, r="DB BC", w="RB")
 
     def build_sh(t):
         for h in (8, 5, 3, 2, 1, 0):
@@ -332,26 +337,29 @@ def rank_program(g, core, T, topo):
     def place(hf, h, j):
         return (T.PD0 if hf == 0 else T.PD1)[:, BASE[h] + j:160:20]
 
-    def bulk(t):
+    def bulk(t, hole):
         PGK = "PG0 PG1 PG2 PG3"
-        act(T.GL[:, 0:1024], T.X[:, 0:4096].indirect(T.LH[:, 0:64]), r="X LH", w="GLa")
-        v(V.tensor_copy, T.GL[:, 1024:2048], T.X[:, 0:4096].indirect(T.LH[:, 64:128]), r="X LH", w="GLb")
-        act(T.GH[:, 0:1024], T.X[:, 0:4096].indirect(T.LH[:, 128:192]), r="X LH", w="GHa")
-        act(T.GH[:, 1024:2048], T.X[:, 0:4096].indirect(T.LH[:, 192:256]), r="X LH", w="GHb")
-        for b_ in range(4):
-            mm(T.PG[:, 512 * b_:512 * b_ + 512], T.IDB[:], T.GL[:, 512 * b_:512 * b_ + 512], r="IDB GL" + "ab"[b_ // 2], w="pg", b="PG%d" % b_)
-        thr(T.N0[:], "N0")
-        if t == 0:
-            consts_late()
-        for hf in range(2):
-            mm(pd(hf, 0, 160), T.ONE[:], T.RB[:], True, False, r="ONE RB", w="pd%d" % hf, b="PD%d" % hf)
+        for b_ in range(2):
+            c, k_ = 512 * b_, "GLa R0a" if b_ else "GLc R0c"
+            act(T.GL[:, c:c + 512], T.X[:, 0:4096].indirect(T.LH[:, 32 * b_:32 * b_ + 32]), r="X LH0", w=k_)
+            c, k_ = 1024 + 512 * b_, "GLb R0b" if b_ else "GLd R0d"
+            v(V.tensor_copy, T.GL[:, c:c + 512], T.X[:, 0:4096].indirect(T.LH[:, 64 + 32 * b_:96 + 32 * b_]), r="X LH0", w=k_)
+        for b_ in range(2):
+            c, k_ = 512 * b_, "a" if b_ else "c"
+            mm(T.PG[:, c:c + 512], T.IDB[:], T.GL[:, c:c + 512], r="IDB GL%s R0%s" % (k_, k_), w="pg", b="PG%d" % b_)
+            c, k_ = 1024 + 512 * b_, "b" if b_ else "d"
+            for j in range(1, 6):
+                mm(T.PG[:, c + j:c + 512:8], T.IDB[:], T.GL[:, c + j:c + 512:8], r="IDB GL%s" % k_, w="pg", b="PG%d" % (2 + b_))
+        act(T.GH[:, 0:1024], T.X[:, 0:4096].indirect(T.LH[:, 128:192]), r="X LH1", w="GHa")
+        act(T.GH[:, 1024:2048], T.X[:, 0:4096].indirect(T.LH[:, 192:256]), r="X LH1", w="GHb")
+        hole()
 
         def low(hf, j):
-            k_ = {(0, 0): 0, (0, 1): 1, (0, 2): 2, (1, 0): 3}.get((hf, j))
             gl = T.GL[:, 1024 * hf + j:1024 * hf + 1024:8]
-            key = "GL%s%s" % ("ab"[hf], " GL0" if j == 0 else "")
-            if k_ is not None:
-                mm(pd(hf, 0, 160), gl, T.CP[:, 160 * k_:160 * k_ + 160], False, False, r=key + cpk, w="pd%d" % hf, b="PD%d" % hf)
+            key = ("R0" if j == 0 else "GL") + "ab"[hf]
+            if j < 4:
+                k_ = 4 * hf + j
+                mm(pd(hf, 0, 160), gl, T.CP[:, 160 * k_:160 * k_ + 160], False, False, r=key + " " + cpk[hf][j], w="pd%d" % hf, b="PD%d" % hf)
                 return
             for h in HS:
                 if h > j and not (h == 8 and hf == 1):
@@ -368,8 +376,10 @@ def rank_program(g, core, T, topo):
         def add(hf, h, j, last=False):
             o = place(hf, h, j)
             if h == 8:
-                mm(o, T.D8[:, 1024 * hf + j:1024 * hf + 1024:8], T.K2[:] if hf == 0 else T.KB[:], False, last,
-                   r=("K2 D8a D8b" + (" D8j" if j == 0 else "")) if hf == 0 else "KB D8c D8d", w="pd%d" % hf, b="PD%d" % hf)
+                if hf == 0:
+                    mm(o, T.D8[:, j:1024:8], T.K2[:], False, last, r="K2 D8a D8b" + (" D8j" if j == 0 else ""), w="pd0", b="PD0")
+                else:
+                    mm(o, T.D8[:, 1024 + 128 * j:1152 + 128 * j], T.KB[:], False, last, r="KB D8x%d" % (0 if j == 0 else 1 if j < 5 else 5), w="pd1", b="PD1")
             else:
                 c = 256 * idx(h, j) + 128 * hf
                 mm(o, T.DL[:, c:c + 128], T.K2[:], False, last, r="K2 DL%d%d" % (h, j), w="pd%d" % hf, b="PD%d" % hf)
@@ -377,64 +387,76 @@ def rank_program(g, core, T, topo):
         def pair(h, j):
             c = 256 * idx(h, j)
             if j == 0:
-                i0, i1, key = T.PG[:, h:2048:8], T.GL[:, 0:2048:8], "GL0"
+                i0, i1, key = T.PG[:, h:2048:8], T.GL[:, 0:2048:8], "R0a R0b"
             elif j + h < 8:
                 i0, i1, key = T.PG[:, j:2048:8], T.GL[:, j + h:2048:8], "GLa GLb"
             else:
                 i0, i1, key = T.PG[:, j:2048:8], T.GH[:, j + h - 8:2048:8], "GHa GHb"
             v(V.tensor_tensor, T.DL[:, c:c + 256], i0, i1, A.max, r="pg " + key, w="DL%d%d" % (h, j), b=PGK)
 
-        for hf in range(2):
-            for rr in range(1, 8):
-                low(hf, rr)
-                high(hf, rr)
+        def sizes(js, B, bk):
+            n = 128 * len(js)
+            for q_, j in enumerate(js):
+                mm(B[:, 128 * q_:128 * q_ + 128], T.IDB[:], T.GL[:, 1024 + j:2048:8], True, False, r="IDB %sb" % ("R0" if j == 0 else "GL"), b=bk)
+                mm(B[:, 128 * q_:128 * q_ + 128], T.NIB[:], T.GH[:, 1024 + j:2048:8], False, True, r="NIB GHb", w="pB" + bk, b=bk)
+            act(T.D8[:, 1024 + 128 * js[0]:1024 + 128 * js[0] + n], B[:, 0:n], F.Abs, r="pB" + bk, w="D8x%d" % js[0], b=bk)
+
         early = ((2, 1), (3, 1), (3, 2), (5, 1), (5, 2))
         for h, j in early:
             pair(h, j)
-            for hf in range(2):
-                add(hf, h, j)
+        sizes((1, 2, 3, 4), T.B4, "B4")
+        sizes((5, 6, 7), T.B5, "B5")
+        v(V.tensor_tensor, T.D8[:, 0:512], T.PG[:, 0:512], T.GH[:, 0:512], A.max, r="pg GHa", w="D8a", b="PG0")
+        if t > 0:
+            v(V.tensor_copy, T.LLU[:], T.MNR[:, 32 * (t - 1) + 16:32 * t], r="MNR%d" % (t - 1), w="LLU")
+            v(V.tensor_scalar, T.S5[:], T.MNR[:, 32 * (t - 1):32 * (t - 1) + 16], 5, None, A.mult, r="MNR%d" % (t - 1), w="S5")
+        act(T.GL[:, 0:2048:8], T.X[:, 0:4096].indirect(T.LLU[:]), r="X LLU GLa GLb", w="R0a R0b R0c R0d")
+        v(V.tensor_tensor, T.D8[:, 512:1024], T.PG[:, 512:1024], T.GH[:, 512:1024], A.max, r="pg GHa", w="D8b", b="PG1")
+        for hf in range(2):
+            if hf == 1:
+                sizes((0,), T.B4, "B4")
+            mm(pd(hf, 0, 160), T.ONE[:], T.RB[:], True, False, r="ONE RB", w="pd%d" % hf, b="PD%d" % hf)
+            for rr in range(1, 8):
+                low(hf, rr)
+                if rr > 3:
+                    high(hf, rr)
         for rr in range(8, 16):
             high(0, rr)
-        for b_ in range(2):
-            v(V.tensor_tensor, T.D8[:, 512 * b_:512 * b_ + 512], T.PG[:, 512 * b_:512 * b_ + 512], T.GH[:, 512 * b_:512 * b_ + 512], A.max, r="pg GHa", w="D8" + "ab"[b_], b="PG%d" % b_)
+        for h, j in early:
+            for hf in range(2):
+                add(hf, h, j)
         for j in range(1, 8):
             add(0, 8, j)
         high(1, 8)
         high(1, 9)
-        if t > 0:
-            v(V.tensor_copy, T.LLU[:], T.MNR[:, 32 * (t - 1) + 16:32 * t], r="MNR%d" % (t - 1), w="LLU")
-            v(V.tensor_scalar, T.S5[:], T.MNR[:, 32 * (t - 1):32 * (t - 1) + 16], 5, None, A.mult, r="MNR%d" % (t - 1), w="S5")
-        act(T.GL[:, 0:2048:8], T.X[:, 0:4096].indirect(T.LLU[:]), r="X LLU", w="GL0 GLa GLb")
         for h, j in ((5, 3), (5, 4)):
             pair(h, j)
             for hf in range(2):
                 add(hf, h, j)
-        for b_, B, bk in ((2, T.B4, "B4"), (3, T.B5, "B5")):
-            mm(B[:], T.IDB[:], T.GL[:, 512 * b_:512 * b_ + 512], True, False, r="IDB GL0 GLb", w="pB", b=bk)
-            mm(B[:], T.NIB[:], T.GH[:, 512 * b_:512 * b_ + 512], False, True, r="NIB GHb", w="pB" + bk, b=bk)
-            act(T.D8[:, 512 * b_:512 * b_ + 512], B[:], F.Abs, r="pB" + bk, w="D8" + "abcd"[b_], b=bk)
         for hf in range(2):
             low(hf, 0)
+        v(V.tensor_tensor, T.D8[:, 0:1024:8], T.GL[:, 0:1024:8], T.GH[:, 0:1024:8], A.max, r="R0a GHa D8a D8b", w="D8j")
+        add(0, 8, 0)
+        for j in range(1, 8):
+            add(1, 8, j)
+        add(1, 8, 0)
         for h in (5, 3, 2, 1):
             pair(h, 0)
             for hf in range(2):
-                add(hf, h, 0)
-        v(V.tensor_tensor, T.D8[:, 0:1024:8], T.GL[:, 0:1024:8], T.GH[:, 0:1024:8], A.max, r="GL0 GHa D8a D8b", w="D8j")
-        add(0, 8, 0, True)
-        for j in range(8):
-            add(1, 8, j, j == 7)
-        v(V.tensor_tensor_scan, T.ZC[:], T.ZR[:], T.GL[:], 0.0, A.mult, A.max, r="ZR GLa GLb GL0", w="ZC")
-        act(T.ZC[:, 5:2048:8], T.GL[:, 0:2048:8], r="GL0 ZC", w="ZC5")
+                add(hf, h, 0, h == 1)
+        v(V.tensor_tensor_scan, T.ZC[:], T.ZR[:], T.GL[:], 0.0, A.mult, A.max, r="ZR GLa GLb R0a R0b", w="ZC")
+        act(T.ZC[:, 5:2048:8], T.GL[:, 0:2048:8], r="R0a R0b ZC", w="ZC5")
 
     def decode(t):
         last = t == TV - 1
         rs = 16 if last else 0
         m1 = 288 * t
-        for hf in range(2):
-            B, bk = (T.B4, "B4") if hf == 0 else (T.B5, "B5")
-            c = 160 * hf
+        halves = ((0, T.B4, "B4", 0), (1, T.B5, "B5", 160))
+        for hf, B, bk, c in halves:
             v(V.tensor_tensor_scan, B[:, 0:160], T.D0[:], pd(hf, 0, 160), 0.0, A.mult, A.max, r="pd%d %s" % (hf, d0k), w="s1%d" % hf, b="PD%d %s" % (hf, bk))
+        for hf, B, bk, c in halves:
             v(V.tensor_tensor, T.E[:, c:c + 160], B[:, 0:160], T.THR[:, c:c + 160], A.is_gt, r="s1%d %s" % (hf, thk), w="E%d" % hf, b=bk)
+        for hf, B, bk, c in halves:
             v(V.tensor_tensor_scan, T.SC2[:, c:c + 160], T.E[:, c:c + 160], T.C2[:], 0.0, A.mult, A.add, r="E%d %s" % (hf, c2k), w="SC%d" % hf)
         v(V.tensor_tensor, T.EK[:], T.SC2[:].indirect(T.LK9[:]), T.ME[:], A.mult, r="SC0 SC1 LK9 ME", w="EK")
         mm(T.PG[:, 0:16], T.IDB[:], T.B8[:], True, False, r="IDB B8", w="p1", b="PG0")
@@ -444,34 +466,36 @@ def rank_program(g, core, T, topo):
             mm(T.PG[:, 512 + 8 * hf:520 + 8 * hf], T.EK[:, 144 * hf + rs:144 * hf + rs + 128], T.K256[:], r="EK K256", w="p2", b="PG1")
         kap = T.SC2[:, 19:320:20]
         v(V.tensor_scalar, T.NH[:], kap, 5, None, A.is_equal, r="SC0 SC1", w="NH")
+        v(V.tensor_scalar, T.DU[:], T.NH[:], 4096, None, A.mult, r="NH", w="DU")
+        v(V.tensor_scalar, T.H1[:], T.NH[:], -6, 1, A.mult, A.add, r="NH", w="H1")
+        v(V.tensor_tensor, T.S5[:], T.S5[:], T.NH[:], A.mult, r="S5 NH", w="S5")
         v(V.tensor_copy, T.L1[:], T.PG[:, 0:16], r="p1", w="L1", b="PG0")
+        v(V.tensor_tensor, T.H[:], T.H1[:], kap, A.add, r="H1 SC0 SC1", w="H")
         v(V.tensor_copy, T.M1S[:, m1:m1 + 128], T.ZC[:].indirect(T.L1[:, 0:8]), r="ZC ZC5 L1", w="Za")
         act(T.M1S[:, m1 + 128:m1 + 256], T.ZC[:].indirect(T.L1[:, 8:16]), r="ZC ZC5 L1", w="Zb")
         act(T.M1S[:, m1 + 256:m1 + 272], T.PG[:, 512:528], r="p2", w="Zc", b="PG1")
         for hf in range(2):
             mm(T.PG[:, 1024 + 8 * hf:1032 + 8 * hf], T.M1S[:, m1 + 128 * hf:m1 + 128 * hf + 128], T.WTB[:], r="Z%s WTB" % "ab"[hf], w="pt", b="PG2")
         mm(T.PG[:, 1536:1552], T.IDB[:], T.B16[:], True, False, r="IDB B16", w="p3", b="PG3")
-        v(V.tensor_scalar, T.H1[:], T.NH[:], -6, 1, A.mult, A.add, r="NH", w="H1")
-        v(V.tensor_tensor, T.S5[:], T.S5[:], T.NH[:], A.mult, r="S5 NH", w="S5")
-        v(V.tensor_tensor, T.H[:], T.H1[:], kap, A.add, r="H1 SC0 SC1", w="H")
-        v(V.tensor_scalar, T.DU[:], T.NH[:], 4096, None, A.mult, r="NH", w="DU")
         v(V.tensor_tensor, T.AD[:], T.S5[:], T.H[:], A.add, r="S5 H", w="AD")
         v(V.tensor_tensor, T.NP[:], T.N1[:], T.H[:], A.subtract, r="N1 H", w="NP")
+        v(V.tensor_tensor, T.SUM[:], T.PG[:, 1024:1040], T.AD[:], A.add, r="pt AD", w="SUM", b="PG2")
         if last:
             v(V.tensor_copy, T.M1S[:, m1 + 272:m1 + 288], T.NP[:], r="NP", w="Zd")
         else:
             v(V.tensor_copy, T.M1S[:, m1 + 272:m1 + 288], T.NP[:].indirect(T.ROT[:, 0:1]), r="NP ROT", w="Zd")
-        v(V.tensor_tensor, T.SUM[:], T.PG[:, 1024:1040], T.AD[:], A.add, r="pt AD", w="SUM", b="PG2")
         v(V.tensor_scalar, T.V15[:], T.SUM[:], 15, None, A.bitwise_and, r="SUM", w="V15")
         v(V.tensor_tensor, T.VV[:], T.V15[:], T.DU[:], A.max, r="V15 DU", w="VV")
         v(V.tensor_tensor, T.EV[:], T.VV[:].indirect(T.LU[:]), T.ME[:, 0:256], A.mult, r="VV LU ME", w="EV")
         for hf in range(2):
             mm(T.PG[:, 1536 + 8 * hf:1544 + 8 * hf], T.EV[:, 128 * hf:128 * hf + 128], T.KB[:], False, hf == 1, r="EV KB", w="p3", b="PG3")
+        v(V.tensor_scalar, T.SI[:], T.SUM[:], 4095, None, A.bitwise_and, r="SUM", w="SI")
+        if not last:
+            v(V.tensor_scalar, T.U[:], T.NP[:], 77, None, A.mult, r="NP", w="U")
+            v(V.tensor_tensor, T.T1[:], T.SI[:], T.SI[:], A.mult, r="SI", w="T1")
         v(V.tensor_copy, T.MLS[:, 16 * t:16 * t + 16], T.PG[:, 1536:1552], r="p3", w="MLS", b="PG3")
         send("M1%d" % t, nxt, T.M1R[:, m1:m1 + 288], T.M1S[:, m1:m1 + 288], r="Za Zb Zc Zd")
         send("ML%d" % t, nxt, T.MLR[:, 16 * t:16 * t + 16], T.MLS[:, 16 * t:16 * t + 16], r="MLS")
-        v(V.tensor_scalar, T.SI[:], T.SUM[:], 4095, None, A.bitwise_and, r="SUM", w="SI")
-        return last
 
     def xupdate(t, a=0, b=16, tag=""):
         cols = T.MLR[:, 16 * t + a:16 * t + b]
@@ -479,6 +503,28 @@ def rank_program(g, core, T, topo):
         v(V.tensor_tensor, T.XT[:, n0:n1], T.X[:].indirect(cols), T.M1R[:, 288 * t + n0:288 * t + n1], A.add, r="X XD MLR%d M1R%d" % (t, t), w="XT")
         v(V.tensor_scalar, T.XU[:, n0:n1], T.XT[:, n0:n1], 0.5, 127.75, A.mult, A.add, r="XT", w="XU")
         v(V.tensor_tensor, T.X[:].indirect(cols), T.XU[:, n0:n1], T.NEG[:, n0:n1], A.add, r="XU NEG MLR%d" % t, w="X XD")
+
+    def first():
+        bound()
+        v(V.memset, T.ONE[:], 1.0, w="ONE")
+        v(V.memset, T.THR[:], -1.0, w="THR")
+        v(V.memset, T.THR[:, 0:320:20], 1000.0, r="THR", w="THR0")
+        thr(T.N0[:], "N0")
+        v(V.memset, T.ZR[:, 0:2048:8], 0.0, r="ZR", w="ZR")
+        v(V.tensor_copy, T.WTF[:], T.WTI[:], r="WTI", w="WTF")
+        v(V.tensor_scalar, T.BI[:], T.IK[:], T.P15[:], None, A.add, r="IK P15", w="BI")
+        act(T.WTB[:], T.KB[:], scale=T.WTF[:], r="KB WTF", w="WTB")
+        act(T.K256[:], T.KB[:], scale=256.0, r="KB", w="K256")
+        act(T.B8[:], T.BI[:], scale=8.0, r="BI", w="B8")
+        act(T.B16[:], T.BI[:], scale=16.0, r="BI", w="B16")
+        v(V.tensor_scalar, T.S5[:], T.SI[:], 5, None, A.mult, r="SI", w="S5")
+
+    def rot_list():
+        v(V.tensor_scalar, T.P15I[:, 2:3], T.P15I[:, 0:1], 8, None, A.bitwise_and, r="P15I", w="P15c")
+        v(V.tensor_scalar, T.P15I[:, 3:4], T.P15I[:, 0:1], -1, None, A.add, r="P15I", w="P15d")
+        v(V.tensor_scalar, T.P15I[:, 3:4], T.P15I[:, 3:4], 7, None, A.bitwise_and, r="P15d", w="P15d")
+        v(V.tensor_tensor, T.P15I[:, 2:3], T.P15I[:, 2:3], T.P15I[:, 3:4], A.add, r="P15c P15d", w="P15c")
+        v(V.tensor_copy, T.ROT[:, 0:1], T.P15I[:, 2:3], r="P15c", w="ROT")
 
     for t in range(TV):
         if t < TV - 1:
@@ -489,36 +535,44 @@ def rank_program(g, core, T, topo):
                 c = 256 * SLOT[h]
                 dma("sh", T.SH[0:128 - h, c:c + 256], T.W2[h:128, 1024:1280], r="W24", w="SA%d SB%d" % (h, h))
             dma("sh2", T.SH[0:128:16, 1280:1536], T.LFR[0:128:16, 1024:1280], r="LFR4 SA0 SB0", w="SHf SHg")
+        bulk(t, first if t == 0 else hole)
         if t == 0:
-            bound()
-        bulk(t)
+            consts_scan()
+            rot_list()
         decode(t)
         if t == TV - 1:
             break
         u = t + 1
         m1 = 288 * t
-        push1(T.NP[:], "NP")
+        push1(T.NP[:], "NP", lambda: v(V.tensor_reduce, T.NS[:], T.NH[:], AxisListType.X, A.add, r="NH", w="NS"))
         v(V.tensor_copy, T.MNS[:, 32 * t:32 * t + 16], T.SI[:].indirect(T.ROT[:, 0:1]), r="SI ROT", w="MNa")
         v(V.tensor_tensor, T.KBI[:], T.M1R[:, m1 + 256:m1 + 272], T.BI[:], A.add, r="M1R%d BI" % t, w="KBI")
         v(V.tensor_copy, T.L2[:], T.KBI[:], r="KBI", w="L2")
         act(T.W2[:, 256 * u:256 * u + 256], T.SH[:].indirect(T.L2[:]), r="L2 " + shk, w="W2%d" % u)
+        mm(T.PG[:, 256:257], T.ONEF[:], T.NS[:], r="ONEF NS", w="pA", b="PG0")
         push2(0)
-        rearr(u)
+        rearr(u, 0)
         push2b("LSN")
-        v(V.tensor_reduce, T.NS[:], T.NH[:], AxisListType.X, A.add, r="NH", w="NS")
-        mm(T.B5[:, 0:1], T.ONEF[:], T.NS[:], r="ONEF NS", w="pA", b="B5")
-        v(V.tensor_scalar, T.AI[:], T.B5[:, 0:1], -1, 2048, A.mult, A.add, r="pA", w="AI", b="B5")
-        v(V.tensor_scalar, T.AJ[:], T.AI[:], 15, None, A.bitwise_and, r="AI", w="AJ")
-        v(V.tensor_scalar, T.BC[:], T.AJ[:], T.THF[:], -1, A.add, A.mult, r="AJ THF", w="BC")
-        bound()
-        v(V.tensor_copy, T.N0[:], T.M1R[:, m1 + 272:m1 + 288], r="M1R%d" % t, w="N0")
-        push3(u)
+        push2w()
+        rearr(u, 1)
+        v(V.tensor_scalar, T.AI[:], T.PG[:, 256:257], -1, 2048, A.mult, A.add, r="pA", w="AI", b="PG0")
         xupdate(t)
-        lists()
+        lists(0)
+        push3()
+        lists(1)
         push4()
-        act(T.MNS[:, 32 * t + 16:32 * t + 32], T.B5[:, 0:16], r="pL", w="MNb", b="B5")
-        send("MN%d" % t, nxt, T.MNR[:, 32 * t:32 * t + 32], T.MNS[:, 32 * t:32 * t + 32], r="MNa MNb")
-        send("LF%d" % u, nx2 if u < 4 else nxt, T.LFR[:, 256 * u:256 * u + 256], T.LF[:, 256 * u:256 * u + 256], r="LF%d" % u)
+        push2f()
+
+        def hole(t=t, u=u, m1=m1):
+            v(V.tensor_copy, T.MNS[:, 32 * t + 16:32 * t + 32], T.B5[:, 0:16], r="pL", w="MNb", b="B5")
+            send("MN%d" % t, nxt, T.MNR[:, 32 * t:32 * t + 32], T.MNS[:, 32 * t:32 * t + 32], r="MNa MNb")
+            push3f(u)
+            send("LF%d" % u, nx2 if u < 4 else nxt, T.LFR[:, 256 * u:256 * u + 256], T.LF[:, 256 * u:256 * u + 256], r="LF%d" % u)
+            v(V.tensor_scalar, T.AJ[:], T.AI[:], 15, None, A.bitwise_and, r="AI", w="AJ")
+            v(V.tensor_copy, T.N0[:], T.M1R[:, m1 + 272:m1 + 288], r="M1R%d" % t, w="N0")
+            v(V.tensor_scalar, T.BC[:], T.AJ[:], T.THF[:], -1, A.add, A.mult, r="AJ THF", w="BC")
+            bound()
+            thr(T.N0[:], "N0")
 
     v(V.tensor_copy, T.SF[:], T.SI[:], r="SI", w="SF")
     v(V.tensor_tensor, T.KBI[:], T.M1S[:, 4 * 288 + 256:4 * 288 + 272], T.BI[:], A.add, r="Zc BI", w="KBI")

@@ -4,6 +4,7 @@ HS = (8, 5, 3, 2, 1)
 BASE = {8: 1, 5: 9, 3: 14, 2: 17, 1: 19}
 SLOT = {1: 0, 2: 1, 3: 2, 5: 4, 8: 7, 0: 5}
 TV = 5
+MAXED = (1, 2, 3)
 PAIRS = [(h, j) for h in (5, 3, 2, 1) for j in range(h)]
 
 SCRATCH = {
@@ -154,10 +155,10 @@ def rank_program(g, core, T, topo):
     dma("small", T.NLI[:], T.nl[:], w="NLI")
     dma("wd", T.WI[1:128, :], T.wd[0:127, :], w="WIa")
     dma("wd", T.WI[0:1, :], T.wd[0:1, :], w="WIb")
-    dma("ls", T.LS[:], T.ls[:], w="LS")
     dma("sm2", T.THI[0:128:16, :], T.th[:], w="THI")
     dma("sm2", T.WTI[:], T.wt[:], w="WTI")
-    dma("x", T.X[:, 0:4096], T.x[:], w="X")
+    dma("x", T.X[:, 0:4096], T.x[:], w="XA XB")
+    dma("ls", T.LS[:], T.ls[:], w="LS")
 
     def iota(out, pat, base, cm, key):
         run("g", g.iota, out, pat, base, cm, w=key)
@@ -236,20 +237,26 @@ def rank_program(g, core, T, topo):
         for hf in range(2):
             mm(T.PG[:, 512 + 128 * hf:640 + 128 * hf], T.RS[:, 144 * hf + sl:144 * hf + sl + 128], T.IDB[:], r="RS IDB", w="pR", b="PG1")
 
-    def push2b(ls):
+    def push2a():
         v(V.tensor_copy, T.CL[:], T.PG[:, 0:16], r="pC", w="CL", b="PG0")
         v(V.tensor_scalar, T.MK[:], T.PG[:, 512:768], T.P15[:], None, A.is_equal, r="pR P15", w="MK", b="PG1")
+
+    def push2b(ls):
         v(V.tensor_tensor, T.MM[:], T[ls][:].indirect(T.CL[:]), T.MK[:], A.mult, r=ls + " CL MK", w="MM")
 
-    def push2w():
+    lwb = {0: (T.B5, 16, "B5"), 1: (T.PG, 1024, "PG2")}
+
+    def push2w(k_=1):
+        B, c, bk = lwb[k_]
         for hf in range(2):
-            mm(T.PG[:, 1024 + 8 * hf:1032 + 8 * hf], T.MM[:, 128 * hf:128 * hf + 128], T.KF[:], r="MM KF", w="pW", b="PG2")
+            mm(B[:, c + 8 * hf:c + 8 + 8 * hf], T.MM[:, 128 * hf:128 * hf + 128], T.KF[:], r="MM KF", w="pW", b=bk)
 
     def push2f():
         mm(T.B5[:, 256:512], T.ROW0[:], T.MM[:], r="MM ROW0", w="pF", b="B5")
 
-    def push3():
-        v(V.tensor_copy, T.LW[:], T.PG[:, 1024:1040], r="pW", w="LW", b="PG2")
+    def push3(k_=1):
+        B, c, bk = lwb[k_]
+        v(V.tensor_copy, T.LW[:], B[:, c:c + 16], r="pW", w="LW", b=bk)
 
     def push3f(t):
         act(T.LF[:, 256 * t:256 * t + 256], T.B5[:, 256:512], r="pF", w="LF%d" % t, b="B5")
@@ -273,45 +280,43 @@ def rank_program(g, core, T, topo):
         src, bk = (T.B4[:, 128:256], "B4") if b_ == 0 else (T.PG[:, 1792:1920], "PG3")
         v(V.tensor_copy, T.LH[:, 128 * b_:128 * b_ + 128], src, r="pH%d" % b_, w="LH%d" % b_, b=bk)
 
-    push2(16)
     rearr(0, 0)
     rearr(0, 1)
+    push2(16)
     lists(0)
-    lists(1)
     act(T.KN[:], T.KB[:], scale=-1.0, r="KB", w="KN")
     act(T.K2[:], T.KB[:], scale=2.0, r="KB", w="K2")
     act(T.NIB[:], T.IDB[:], scale=-1.0, r="IDB", w="NIB")
     act(T.ROW0[:, 0:128:16], T.KF[:], r="KF", w="ROW0")
-    cpk = [["CP"] * 4, ["CP"] * 4]
-    for rr in (1, 2, 3, 0):
-        for hf in range(2):
-            for h in HS[hf:]:
-                for j in (rr, rr - h):
-                    if 0 <= j < h:
-                        key, c = "CP%d%d%d" % (hf, rr, h), 160 * (4 * hf + rr) + BASE[h] + j
-                        act(T.CP[:, c:160 * (4 * hf + rr) + 160:20], T.KN[:], r="KN CP", w=key)
-                        cpk[hf][rr] += " " + key
+    cpk = ["CP"] * 5
+    for k_ in (1, 2, 3, 0, 4):
+        rr = k_ % 4
+        for h in HS[k_ // 4:]:
+            for j in (rr, rr - h):
+                if 0 <= j < h:
+                    key, c = "CP%d%d" % (k_, h), 160 * k_ + BASE[h] + j
+                    act(T.CP[:, c:160 * k_ + 160:20], T.KN[:], r="KN CP", w=key)
+                    cpk[k_] += " " + key
     act(T.SH[:, 768:1024], T.W2[:, 0:256], scale=0.0, r="W20", w="SH3")
     act(T.SH[:, 1536:1792], T.W2[:, 0:256], scale=0.0, r="W20", w="SH6")
     act(T.ONEF[:], T.IDF[:], F.Identity, scale=0.0, bias=1.0, r="IDF", w="ONEF")
     act(T.NEG[:], T.W2[:, 0:256], F.Identity, scale=0.0, bias=-128.0, r="W20", w="NEG")
-    push2b("LS")
-    push2w()
-    push3()
-    push4()
-    v(V.tensor_copy, T.LLU[:], T.B5[:, 0:16], r="pL", w="LLU", b="B5")
-    push2f()
-    push3f(0)
+    push2a()
     send("LS", prv, T.LSN[:], T.LS[:], r="LS")
-    send("LF0", nxt, T.LFR[:, 0:256], T.LF[:, 0:256], r="LF0")
+
+    def first0():
+        lists(1)
+
     v(V.tensor_copy, T.THF[:], T.THI[:], r="THI", w="THF")
     v(V.tensor_scalar, T.DB[:], T.I20[:], 0, None, A.is_equal, r="I20", w="DB")
     v(V.tensor_scalar, T.BC[:], T.THF[:], -1, None, A.mult, r="THF", w="BC")
 
     shk = "SH3 SH6 SHf SHg " + " ".join("SA%d SB%d" % (h, h) for h in (8, 5, 3, 2, 1, 0))
 
-    def thr(ncol, nkey):
+    def n1(ncol, nkey):
         v(V.tensor_scalar, T.N1[:], ncol, 1, 16, A.add, A.min, r=nkey, w="N1")
+
+    def thr():
         for h in HS:
             e = BASE[h] + h - 1
             v(V.tensor_scalar, T.THR[:, e:320:20], T.N1[:], 0.5 - 2 * h, 0.0, A.add, A.min, r="N1 THR", w="THR%d" % e)
@@ -337,29 +342,29 @@ def rank_program(g, core, T, topo):
     def place(hf, h, j):
         return (T.PD0 if hf == 0 else T.PD1)[:, BASE[h] + j:160:20]
 
-    def bulk(t, hole):
+    def bulk(t, mid, hole):
         PGK = "PG0 PG1 PG2 PG3"
+        v(V.tensor_copy, T.GL[:, 1024:1536], T.X[:, 0:4096].indirect(T.LH[:, 64:96]), r="XA XB LH0", w="GLd R0d")
+        for c, k_ in ((0, "c"), (512, "a"), (1536, "b")):
+            act(T.GL[:, c:c + 512], T.X[:, 0:4096].indirect(T.LH[:, c // 16:c // 16 + 32]), r="XA XB LH0", w="GL%s R0%s" % (k_, k_))
         for b_ in range(2):
-            c, k_ = 512 * b_, "GLa R0a" if b_ else "GLc R0c"
-            act(T.GL[:, c:c + 512], T.X[:, 0:4096].indirect(T.LH[:, 32 * b_:32 * b_ + 32]), r="X LH0", w=k_)
-            c, k_ = 1024 + 512 * b_, "GLb R0b" if b_ else "GLd R0d"
-            v(V.tensor_copy, T.GL[:, c:c + 512], T.X[:, 0:4096].indirect(T.LH[:, 64 + 32 * b_:96 + 32 * b_]), r="X LH0", w=k_)
-        for b_ in range(2):
+            if b_ == 1:
+                mid()
             c, k_ = 512 * b_, "a" if b_ else "c"
             mm(T.PG[:, c:c + 512], T.IDB[:], T.GL[:, c:c + 512], r="IDB GL%s R0%s" % (k_, k_), w="pg", b="PG%d" % b_)
             c, k_ = 1024 + 512 * b_, "b" if b_ else "d"
             for j in range(1, 6):
                 mm(T.PG[:, c + j:c + 512:8], T.IDB[:], T.GL[:, c + j:c + 512:8], r="IDB GL%s" % k_, w="pg", b="PG%d" % (2 + b_))
-        act(T.GH[:, 0:1024], T.X[:, 0:4096].indirect(T.LH[:, 128:192]), r="X LH1", w="GHa")
-        act(T.GH[:, 1024:2048], T.X[:, 0:4096].indirect(T.LH[:, 192:256]), r="X LH1", w="GHb")
+        act(T.GH[:, 0:1024], T.X[:, 0:4096].indirect(T.LH[:, 128:192]), r="XA XB LH1", w="GHa")
+        act(T.GH[:, 1024:2048], T.X[:, 0:4096].indirect(T.LH[:, 192:256]), r="XA XB LH1", w="GHb")
         hole()
 
         def low(hf, j):
             gl = T.GL[:, 1024 * hf + j:1024 * hf + 1024:8]
             key = ("R0" if j == 0 else "GL") + "ab"[hf]
             if j < 4:
-                k_ = 4 * hf + j
-                mm(pd(hf, 0, 160), gl, T.CP[:, 160 * k_:160 * k_ + 160], False, False, r=key + " " + cpk[hf][j], w="pd%d" % hf, b="PD%d" % hf)
+                k_ = 4 if hf == 1 and j == 0 else j
+                mm(pd(hf, 0, 160), gl, T.CP[:, 160 * k_:160 * k_ + 160], False, False, r=key + " " + cpk[k_], w="pd%d" % hf, b="PD%d" % hf)
                 return
             for h in HS:
                 if h > j and not (h == 8 and hf == 1):
@@ -368,7 +373,7 @@ def rank_program(g, core, T, topo):
         def high(hf, rr):
             for h in HS:
                 j = rr - h
-                if 0 <= j < h and not (h == 8 and hf == 1):
+                if 0 <= j < h and not (h == 8 and hf == 1 and j not in MAXED):
                     src, key = (T.GL, "GL") if rr < 8 else (T.GH, "GH")
                     o = 1024 * hf + rr % 8
                     mm(place(hf, h, j), src[:, o:1024 * hf + 1024:8], T.KN[:], False, False, r=key + "ab"[hf] + " KN", w="pd%d" % hf, b="PD%d" % hf)
@@ -379,7 +384,8 @@ def rank_program(g, core, T, topo):
                 if hf == 0:
                     mm(o, T.D8[:, j:1024:8], T.K2[:], False, last, r="K2 D8a D8b" + (" D8j" if j == 0 else ""), w="pd0", b="PD0")
                 else:
-                    mm(o, T.D8[:, 1024 + 128 * j:1152 + 128 * j], T.KB[:], False, last, r="KB D8x%d" % (0 if j == 0 else 1 if j < 5 else 5), w="pd1", b="PD1")
+                    mm(o, T.D8[:, 1024 + 128 * j:1152 + 128 * j], T.K2[:] if j in MAXED else T.KB[:], False, last,
+                       r="K2 D8y%d" % j if j in MAXED else "KB D8x%d" % min(j, 4), w="pd1", b="PD1")
             else:
                 c = 256 * idx(h, j) + 128 * hf
                 mm(o, T.DL[:, c:c + 128], T.K2[:], False, last, r="K2 DL%d%d" % (h, j), w="pd%d" % hf, b="PD%d" % hf)
@@ -401,25 +407,38 @@ def rank_program(g, core, T, topo):
                 mm(B[:, 128 * q_:128 * q_ + 128], T.NIB[:], T.GH[:, 1024 + j:2048:8], False, True, r="NIB GHb", w="pB" + bk, b=bk)
             act(T.D8[:, 1024 + 128 * js[0]:1024 + 128 * js[0] + n], B[:, 0:n], F.Abs, r="pB" + bk, w="D8x%d" % js[0], b=bk)
 
+        def row0():
+            act(T.GL[:, 0:2048:8], T.X[:, 0:4096].indirect(T.LLU[:]), r="XA XB LLU GLa GLb", w="R0a R0b R0c R0d")
+
         early = ((2, 1), (3, 1), (3, 2), (5, 1), (5, 2))
         for h, j in early:
             pair(h, j)
-        sizes((1, 2, 3, 4), T.B4, "B4")
-        sizes((5, 6, 7), T.B5, "B5")
         v(V.tensor_tensor, T.D8[:, 0:512], T.PG[:, 0:512], T.GH[:, 0:512], A.max, r="pg GHa", w="D8a", b="PG0")
         if t > 0:
             v(V.tensor_copy, T.LLU[:], T.MNR[:, 32 * (t - 1) + 16:32 * t], r="MNR%d" % (t - 1), w="LLU")
             v(V.tensor_scalar, T.S5[:], T.MNR[:, 32 * (t - 1):32 * (t - 1) + 16], 5, None, A.mult, r="MNR%d" % (t - 1), w="S5")
-        act(T.GL[:, 0:2048:8], T.X[:, 0:4096].indirect(T.LLU[:]), r="X LLU GLa GLb", w="R0a R0b R0c R0d")
-        v(V.tensor_tensor, T.D8[:, 512:1024], T.PG[:, 512:1024], T.GH[:, 512:1024], A.max, r="pg GHa", w="D8b", b="PG1")
+            row0()
+        else:
+            push2b("LS")
         for hf in range(2):
             if hf == 1:
-                sizes((0,), T.B4, "B4")
+                if t == 0:
+                    push2w(0)
+                    push3(0)
+                    push4()
+                v(V.tensor_tensor, T.D8[:, 512:1024], T.PG[:, 512:1024], T.GH[:, 512:1024], A.max, r="pg GHa", w="D8b", b="PG1")
             mm(pd(hf, 0, 160), T.ONE[:], T.RB[:], True, False, r="ONE RB", w="pd%d" % hf, b="PD%d" % hf)
             for rr in range(1, 8):
                 low(hf, rr)
                 if rr > 3:
                     high(hf, rr)
+        if t == 0:
+            v(V.tensor_copy, T.LLU[:], T.B5[:, 0:16], r="pL", w="LLU", b="B5")
+            row0()
+        sizes((4, 5, 6, 7), T.B4, "B4")
+        sizes((0,), T.B5, "B5")
+        for j in MAXED:
+            v(V.tensor_tensor, T.D8[:, 1024 + 128 * j:1152 + 128 * j], T.PG[:, 1024 + j:2048:8], T.GH[:, 1024 + j:2048:8], A.max, r="pg GHb", w="D8y%d" % j, b="PG2 PG3")
         for rr in range(8, 16):
             high(0, rr)
         for h, j in early:
@@ -427,8 +446,8 @@ def rank_program(g, core, T, topo):
                 add(hf, h, j)
         for j in range(1, 8):
             add(0, 8, j)
-        high(1, 8)
-        high(1, 9)
+        for rr in (8, 9) + tuple(8 + j for j in MAXED if j > 1):
+            high(1, rr)
         for h, j in ((5, 3), (5, 4)):
             pair(h, j)
             for hf in range(2):
@@ -444,6 +463,10 @@ def rank_program(g, core, T, topo):
             pair(h, 0)
             for hf in range(2):
                 add(hf, h, 0, h == 1)
+        if t == 0:
+            push2f()
+            push3f(0)
+            send("LF0", nxt, T.LFR[:, 0:256], T.LF[:, 0:256], r="LF0")
         v(V.tensor_tensor_scan, T.ZC[:], T.ZR[:], T.GL[:], 0.0, A.mult, A.max, r="ZR GLa GLb R0a R0b", w="ZC")
         act(T.ZC[:, 5:2048:8], T.GL[:, 0:2048:8], r="R0a R0b ZC", w="ZC5")
 
@@ -497,19 +520,19 @@ def rank_program(g, core, T, topo):
         send("M1%d" % t, nxt, T.M1R[:, m1:m1 + 288], T.M1S[:, m1:m1 + 288], r="Za Zb Zc Zd")
         send("ML%d" % t, nxt, T.MLR[:, 16 * t:16 * t + 16], T.MLS[:, 16 * t:16 * t + 16], r="MLS")
 
-    def xupdate(t, a=0, b=16, tag=""):
-        cols = T.MLR[:, 16 * t + a:16 * t + b]
-        n0, n1 = 16 * a, 16 * b
-        v(V.tensor_tensor, T.XT[:, n0:n1], T.X[:].indirect(cols), T.M1R[:, 288 * t + n0:288 * t + n1], A.add, r="X XD MLR%d M1R%d" % (t, t), w="XT")
-        v(V.tensor_scalar, T.XU[:, n0:n1], T.XT[:, n0:n1], 0.5, 127.75, A.mult, A.add, r="XT", w="XU")
-        v(V.tensor_tensor, T.X[:].indirect(cols), T.XU[:, n0:n1], T.NEG[:, n0:n1], A.add, r="XU NEG MLR%d" % t, w="X XD")
+    def xupdate(t, cols, lo, e0, e1, ck, xk):
+        win = T.X[:, lo:8192]
+        v(V.tensor_tensor, T.XT[:, e0:e1], win.indirect(cols), T.M1R[:, 288 * t + e0:288 * t + e1], A.add, r="M1R%d %s %s" % (t, ck, xk), w="XT")
+        v(V.tensor_scalar, T.XU[:, e0:e1], T.XT[:, e0:e1], 0.5, 127.75, A.mult, A.add, r="XT", w="XU")
+        v(V.tensor_tensor, win.indirect(cols), T.XU[:, e0:e1], T.NEG[:, e0:e1], A.add, r="XU NEG " + ck, w=xk)
 
     def first():
         bound()
         v(V.memset, T.ONE[:], 1.0, w="ONE")
         v(V.memset, T.THR[:], -1.0, w="THR")
         v(V.memset, T.THR[:, 0:320:20], 1000.0, r="THR", w="THR0")
-        thr(T.N0[:], "N0")
+        n1(T.N0[:], "N0")
+        thr()
         v(V.memset, T.ZR[:, 0:2048:8], 0.0, r="ZR", w="ZR")
         v(V.tensor_copy, T.WTF[:], T.WTI[:], r="WTI", w="WTF")
         v(V.tensor_scalar, T.BI[:], T.IK[:], T.P15[:], None, A.add, r="IK P15", w="BI")
@@ -535,7 +558,7 @@ def rank_program(g, core, T, topo):
                 c = 256 * SLOT[h]
                 dma("sh", T.SH[0:128 - h, c:c + 256], T.W2[h:128, 1024:1280], r="W24", w="SA%d SB%d" % (h, h))
             dma("sh2", T.SH[0:128:16, 1280:1536], T.LFR[0:128:16, 1024:1280], r="LFR4 SA0 SB0", w="SHf SHg")
-        bulk(t, first if t == 0 else hole)
+        bulk(t, *((first0, first) if t == 0 else (mid, hole)))
         if t == 0:
             consts_scan()
             rot_list()
@@ -552,27 +575,31 @@ def rank_program(g, core, T, topo):
         mm(T.PG[:, 256:257], T.ONEF[:], T.NS[:], r="ONEF NS", w="pA", b="PG0")
         push2(0)
         rearr(u, 0)
+        push2a()
         push2b("LSN")
         push2w()
         rearr(u, 1)
-        v(V.tensor_scalar, T.AI[:], T.PG[:, 256:257], -1, 2048, A.mult, A.add, r="pA", w="AI", b="PG0")
-        xupdate(t)
-        lists(0)
-        push3()
-        lists(1)
-        push4()
         push2f()
+        v(V.tensor_scalar, T.AI[:], T.PG[:, 256:257], -1, 2048, A.mult, A.add, r="pA", w="AI", b="PG0")
+        xupdate(t, T.MLR[:, 16 * t:16 * t + 16], 0, 0, 256, "MLR%d" % t, "XA XB XD")
+        lists(0)
 
-        def hole(t=t, u=u, m1=m1):
+        push3()
+
+        def mid(m1=m1):
+            lists(1)
+            push4()
+            v(V.tensor_scalar, T.AJ[:], T.AI[:], 15, None, A.bitwise_and, r="AI", w="AJ")
+            n1(T.M1R[:, m1 + 272:m1 + 288], "M1R%d" % (m1 // 288))
+
+        def hole(t=t, u=u):
             v(V.tensor_copy, T.MNS[:, 32 * t + 16:32 * t + 32], T.B5[:, 0:16], r="pL", w="MNb", b="B5")
             send("MN%d" % t, nxt, T.MNR[:, 32 * t:32 * t + 32], T.MNS[:, 32 * t:32 * t + 32], r="MNa MNb")
             push3f(u)
             send("LF%d" % u, nx2 if u < 4 else nxt, T.LFR[:, 256 * u:256 * u + 256], T.LF[:, 256 * u:256 * u + 256], r="LF%d" % u)
-            v(V.tensor_scalar, T.AJ[:], T.AI[:], 15, None, A.bitwise_and, r="AI", w="AJ")
-            v(V.tensor_copy, T.N0[:], T.M1R[:, m1 + 272:m1 + 288], r="M1R%d" % t, w="N0")
             v(V.tensor_scalar, T.BC[:], T.AJ[:], T.THF[:], -1, A.add, A.mult, r="AJ THF", w="BC")
+            thr()
             bound()
-            thr(T.N0[:], "N0")
 
     v(V.tensor_copy, T.SF[:], T.SI[:], r="SI", w="SF")
     v(V.tensor_tensor, T.KBI[:], T.M1S[:, 4 * 288 + 256:4 * 288 + 272], T.BI[:], A.add, r="Zc BI", w="KBI")
@@ -587,8 +614,11 @@ def rank_program(g, core, T, topo):
     v(V.tensor_scalar, T.MK[:], T.PG[:, 512:768], T.P15[:], None, A.is_gt, r="pR P15", w="MK", b="PG1")
     v(V.tensor_tensor, T.YW[:], T.SH[:].indirect(T.L2[:]), T.MK[:], A.mult, r="L2 MK " + shk, w="YW")
     dma("oyw", T.yw[:], T.YW[:], r="YW")
-    xupdate(4)
-    dma("oyx", T.yx[:], T.X[:, 0:4096], r="X")
+    xupdate(4, T.MLR[:, 64:72], 0, 0, 128, "MLR4", "XA XB XD")
+    dma("oyx", T.yx[:, 0:2048], T.X[:, 0:2048], r="XA")
+    v(V.tensor_scalar, T.CL[:, 0:8], T.MLR[:, 72:80], -2048, None, A.add, r="MLR4", w="CL")
+    xupdate(4, T.CL[:, 0:8], 2048, 128, 256, "CL", "XB XD")
+    dma("oyx", T.yx[:, 2048:4096], T.X[:, 2048:4096], r="XB")
     act(T.YN[:], T.PG[0:8, 0:256], r="pN", w="YN", b="PG0")
     act(T.YS[:], T.PG[0:8, 1024:1280], r="pS", w="YS", b="PG2")
     dma("oyn", T.yn[:], T.YN[:], r="YN")

from concourse.mybir import AluOpType as A, AxisListType, ActivationFunctionType as F

HS = (8, 5, 3, 2, 1)
BASE = {8: 1, 5: 9, 3: 14, 2: 17, 1: 19}
SLOT = {1: 0, 2: 1, 3: 2, 5: 4, 8: 7, 0: 5}
TV = 5
MAXED = (1, 2, 3)
PAIRS = [(h, j) for h in (5, 3, 2, 1) for j in range(h)]

SCRATCH = {
    "X": ("sbuf", [128, 8192], "bfloat16"), "LS": ("sbuf", [128, 1024], "int32"), "LSN": ("sbuf", [128, 1024], "int32"),
    "SH": ("sbuf", [128, 2048], "float32"), "GL": ("sbuf", [128, 2048], "bfloat16"), "GH": ("sbuf", [128, 2048], "bfloat16"),
    "D8": ("sbuf", [128, 2048], "bfloat16"), "DL": ("sbuf", [128, 11 * 256], "bfloat16"), "ZC": ("sbuf", [128, 2048], "bfloat16"),
    "ZR": ("sbuf", [128, 2048], "bfloat16"), "NEG": ("sbuf", [128, 256], "bfloat16"),
    "M1S": ("sbuf", [128, 5 * 288], "bfloat16"), "M1R": ("sbuf", [128, 5 * 288], "bfloat16"),
    "MLS": ("sbuf", [128, 5 * 16], "uint16"), "MLR": ("sbuf", [128, 5 * 16], "uint16"),
    "MNS": ("sbuf", [128, 5 * 32], "float32"), "MNR": ("sbuf", [128, 5 * 32], "float32"),
    "W2": ("sbuf", [128, 5 * 256], "float32"), "W2R": ("sbuf", [128, 5 * 256], "float32"),
    "LF": ("sbuf", [128, 5 * 256], "float32"), "LFR": ("sbuf", [128, 5 * 256], "float32"),
    "IDB": ("sbuf", [128, 128], "bfloat16"), "NIB": ("sbuf", [128, 128], "bfloat16"), "IDF": ("sbuf", [128, 128], "float32"),
    "ONE": ("sbuf", [128, 128], "bfloat16"), "ONEF": ("sbuf", [128, 128], "float32"), "ROW0": ("sbuf", [128, 128], "float32"),
    "RA": ("sbuf", [128, 512], "float32"), "ME": ("sbuf", [128, 288], "float32"),
    "KB": ("sbuf", [128, 8], "bfloat16"), "KF": ("sbuf", [128, 8], "float32"), "K256": ("sbuf", [128, 8], "bfloat16"),
    "K2": ("sbuf", [128, 8], "bfloat16"), "KN": ("sbuf", [128, 8], "bfloat16"), "WTB": ("sbuf", [128, 8], "bfloat16"),
    "CP": ("sbuf", [128, 1280], "bfloat16"), "DB": ("sbuf", [128, 160], "bfloat16"), "RB": ("sbuf", [128, 160], "bfloat16"),
    "D0": ("sbuf", [128, 160], "bfloat16"), "C2": ("sbuf", [128, 160], "bfloat16"), "THR": ("sbuf", [128, 320], "float32"),
    "E": ("sbuf", [128, 320], "bfloat16"), "SC2": ("sbuf", [128, 320], "bfloat16"),
    "EK": ("sbuf", [128, 288], "bfloat16"), "EC": ("sbuf", [128, 288], "float32"), "RS": ("sbuf", [128, 288], "bfloat16"),
    "EV": ("sbuf", [128, 256], "bfloat16"), "EL": ("sbuf", [128, 256], "float32"),
    "LS9": ("sbuf", [128, 18], "uint16"), "LK9": ("sbuf", [128, 18], "uint16"), "LU": ("sbuf", [128, 16], "uint16"), "ROT": ("sbuf", [128, 2], "uint16"),
    "BI": ("sbuf", [128, 16], "float32"), "B8": ("sbuf", [128, 16], "bfloat16"), "B16": ("sbuf", [128, 16], "bfloat16"),
    "II": ("sbuf", [128, 128], "int32"), "IM": ("sbuf", [128, 288], "int32"), "IG": ("sbuf", [128, 8], "int32"), "I20": ("sbuf", [128, 160], "int32"),
    "IP": ("sbuf", [128, 4], "int32"), "IK": ("sbuf", [128, 16], "int32"), "I9": ("sbuf", [128, 18], "int32"), "IU": ("sbuf", [128, 16], "int32"),
    "P15": ("sbuf", [128, 1], "float32"), "PB": ("sbuf", [128, 2], "float32"), "P15I": ("sbuf", [128, 4], "int32"),
    "SDI": ("sbuf", [8, 256], "int32"), "NLI": ("sbuf", [8, 256], "int32"), "SDF": ("sbuf", [8, 256], "float32"), "NLF": ("sbuf", [8, 256], "float32"),
    "WTI": ("sbuf", [128, 1], "int32"), "WTF": ("sbuf", [128, 1], "float32"), "THI": ("sbuf", [128, 1], "int32"), "THF": ("sbuf", [128, 1], "float32"),
    "WI": ("sbuf", [128, 256], "int32"), "LH": ("sbuf", [128, 256], "uint16"), "L1": ("sbuf", [128, 16], "uint16"), "L2": ("sbuf", [128, 16], "uint16"),
    "LLU": ("sbuf", [128, 16], "uint16"), "CL": ("sbuf", [128, 16], "uint16"), "KBI": ("sbuf", [128, 16], "int32"),
    "N0": ("sbuf", [128, 16], "float32"), "N1": ("sbuf", [128, 16], "float32"), "NP": ("sbuf", [128, 16], "float32"),
    "NH": ("sbuf", [128, 16], "float32"), "H": ("sbuf", [128, 16], "float32"), "H1": ("sbuf", [128, 16], "float32"),
    "S5": ("sbuf", [128, 16], "float32"), "AD": ("sbuf", [128, 16], "float32"), "DU": ("sbuf", [128, 16], "int32"),
    "SUM": ("sbuf", [128, 16], "int32"), "V15": ("sbuf", [128, 16], "int32"), "VV": ("sbuf", [128, 16], "int32"), "SI": ("sbuf", [128, 16], "int32"),
    "S15": ("sbuf", [128, 16], "int32"), "T1": ("sbuf", [128, 16], "int32"), "T2": ("sbuf", [128, 16], "int32"), "U": ("sbuf", [128, 16], "int32"), "CI": ("sbuf", [128, 16], "int32"),
    "MK": ("sbuf", [128, 256], "float32"), "MM": ("sbuf", [128, 256], "float32"), "LW": ("sbuf", [128, 16], "float32"),
    "XT": ("sbuf", [128, 256], "bfloat16"), "XU": ("sbuf", [128, 256], "bfloat16"),
    "NS": ("sbuf", [128, 1], "float32"), "AI": ("sbuf", [128, 1], "int32"), "BC": ("sbuf", [128, 1], "float32"), "AJ": ("sbuf", [128, 1], "int32"),
    "YW": ("sbuf", [128, 256], "float32"), "YN": ("sbuf", [8, 256], "float32"), "YS": ("sbuf", [8, 256], "float32"), "SF": ("sbuf", [128, 16], "float32"),
    "PG": ("psum", [128, 2048], "float32"), "B4": ("psum", [128, 512], "float32"), "B5": ("psum", [128, 512], "float32"),
    "PD0": ("psum", [128, 512], "float32"), "PD1": ("psum", [128, 512], "float32"),
}
_ARR = ["%s%d" % (n, t) for n in ("M1", "ML", "MN", "W2", "LF") for t in range(TV)] + ["LS"]
_DMA = ["small", "sm2", "ls", "wd", "x", "sh", "sh2", "oyx", "oyw", "oyn"]
SEMAPHORES = ["qv", "qa", "qp", "qg", "loc"] + ["r" + n for n in _ARR] + ["d" + n for n in _DMA]


def rank_program(g, core, T, topo):
    rank = T.rank_of(core)
    if rank is None:
        return
    N = len(T.cores)
    nxt, nx2, prv = T.cores[(rank + 1) % N], T.cores[(rank + 2) % N], T.cores[(rank - 1) % N]
    V, P, S = g.vector, g.tensor, g.scalar
    Q = {"v": V, "a": S, "p": P, "g": g, "s": g.sync}

    tot = {}
    known = {q: {} for q in Q}
    lastw, readers, banks, ops = {}, {}, {}, []

    def need(q, deps):
        for o in sorted(deps, reverse=True):
            sem, val, snap, dma = ops[o]
            if known[q].get(sem, 0) >= val:
                continue
            if dma:
                val = tot[sem]
            Q[q].wait_ge(T.sem[sem], val)
            for s_, v_ in snap.items():
                known[q][s_] = max(known[q].get(s_, 0), v_)
            known[q][sem] = val

    def deps_of(q, r, w, b):
        d = set()
        for k in r:
            d.update(lastw.get(k, ()))
        for k in w:
            d.update(lastw.get(k, ()))
            d.update(readers.get(k, ()))
        for k in b:
            d.update(o for q_, o in banks.get(k, {}).items() if q_ != q)
        return d

    def note(q, sem, inc, r, w, b, dma=False):
        tot[sem] = tot.get(sem, 0) + inc
        o = len(ops)
        ops.append((sem, tot[sem], dict(known[q]) if q else {}, dma))
        for k in w:
            lastw[k] = [o]
            readers[k] = []
        for k in r:
            readers.setdefault(k, []).append(o)
        for k in b:
            banks.setdefault(k, {})[q] = o
        return o

    def run(q, fn, *a, r="", w="", b="", **k):
        r, w, b = r.split(), w.split(), b.split()
        need(q, deps_of(q, r, w, b))
        sem = "q" + q
        fn(*a, **k).then_inc(T.sem[sem], 1)
        note(q, sem, 1, r, w, b)

    def v(fn, *a, **k):
        run("v", fn, *a, **k)

    def act(out, in_, func=F.Copy, r="", w="", b="", **k):
        run("a", S.activation, out, in_, func, r=r, w=w, b=b, **k)

    def mm(out, l, rh, start=True, stop=True, r="", w="", b=""):
        r, w, b = r.split(), w.split(), b.split()
        need("p", deps_of("p", r, [], b))
        P.matmul(out, l, rh, start, stop).then_inc(T.sem.qp, 1)
        note("p", "qp", 1, r, w, b)

    def dma(sem, out, in_, r="", w=""):
        r, w = r.split(), w.split()
        need("s", deps_of("s", r, w, []))
        g.sync.dma_start(out, in_).then_inc(T.sem["d" + sem], 16)
        note("s", "d" + sem, 16, r, w, [], True)

    def send(name, dst, out, in_, r=""):
        r = r.split()
        need("g", deps_of("g", r, [], []))
        rid, pid = topo.addr(dst)[:2]
        g.remote_dma(out, in_, T.sem["r" + name], T.sem.loc, pid, rid, topo.mask(core, dst))
        note("g", "loc", len(topo.engines(core, dst)), [], [], [])

    def arrive(name, src, key):
        n = len(topo.engines(src, core))
        tot["r" + name] = n
        lastw[key] = [len(ops)]
        ops.append(("r" + name, n, {}, False))

    p2 = T.cores[(rank - 2) % N]
    for t in range(TV):
        arrive("M1%d" % t, prv, "M1R%d" % t)
        arrive("ML%d" % t, prv, "MLR%d" % t)
        if t < 4:
            arrive("MN%d" % t, prv, "MNR%d" % t)
            arrive("W2%d" % t, prv, "W2R%d" % t)
        arrive("LF%d" % t, prv if t in (0, 4) else p2, "LFR%d" % t)
    arrive("LS", nxt, "LSN")

    v(V.memset, T.THI[:], 0, w="THI")
    dma("small", T.SDI[:], T.sd[:], w="SDI")
    dma("small", T.NLI[:], T.nl[:], w="NLI")
    dma("wd", T.WI[1:128, :], T.wd[0:127, :], w="WIa")
    dma("wd", T.WI[0:1, :], T.wd[0:1, :], w="WIb")
    dma("sm2", T.THI[0:128:16, :], T.th[:], w="THI")
    dma("sm2", T.WTI[:], T.wt[:], w="WTI")
    dma("x", T.X[:, 0:4096], T.x[:], w="XA XB")
    dma("ls", T.LS[:], T.ls[:], w="LS")

    def iota(out, pat, base, cm, key):
        run("g", g.iota, out, pat, base, cm, w=key)
    iota(T.II[:], [[-1, 128]], 0, 1, "II")
    iota(T.IG[:], [[-16, 8]], 0, 1, "IG")
    iota(T.IP[:], [[0, 4]], 0, 1, "IP")
    iota(T.I9[:, 1:9], [[1, 8]], 0, 0, "I9a")
    iota(T.I9[:, 10:18], [[1, 8]], 8, 0, "I9b")
    iota(T.I9[:, 0:1], [[1, 1]], 7, 0, "I9c")
    iota(T.I9[:, 9:10], [[1, 1]], 15, 0, "I9d")
    iota(T.IM[:], [[0, 18], [-1, 16]], 0, 1, "IM")
    iota(T.IU[:], [[1, 16]], 0, 0, "IU")
    iota(T.IK[:], [[16, 16]], 0, 0, "IK")
    iota(T.I20[:], [[-16, 8], [0, 20]], 0, 1, "I20")
    v(V.memset, T.ZR[:], 1.0, w="ZR")
    act(T.CP[:], T.ZR[:, 0:1280], scale=0.0, r="ZR", w="CP")
    for c in (4096, 6144):
        act(T.X[:, c:c + 2048], T.ZR[:], scale=0.0, r="ZR", w="XD")
    d0k = "D0 " + " ".join("D0%d" % q_ for q_ in (0, 1, 9, 14, 17, 19))
    c2k = "C2 C20 C28 C213 C216 C218"

    def consts_scan():
        v(V.memset, T.D0[:], 1.0, w="D0")
        v(V.memset, T.C2[:], 0.0, w="C2")
        for q_ in (0, 1, 9, 14, 17, 19):
            v(V.memset, T.D0[:, q_:160:20], 0.0, r="D0", w="D0%d" % q_)
        for q_, c in ((0, -2.0), (8, 3.0), (13, 2.0), (16, 1.0), (18, 1.0)):
            v(V.memset, T.C2[:, q_:160:20], c, r="C2", w="C2%d" % q_)

    v(V.tensor_scalar, T.IDF[:], T.II[:], 0, None, A.is_equal, r="II", w="IDF")
    v(V.tensor_scalar, T.P15I[:, 1:2], T.IP[:, 0:1], 3, 1, A.arith_shift_right, A.bitwise_and, r="IP", w="P15b")
    v(V.tensor_copy, T.PB[:, 1:2], T.P15I[:, 1:2], r="P15b", w="PB1")
    v(V.tensor_scalar, T.PB[:, 0:1], T.P15I[:, 1:2], -1, 1, A.mult, A.add, r="P15b", w="PB0")
    for b_ in range(2):
        for w_ in range(2):
            c = 128 * (2 * b_ + w_)
            v(V.tensor_scalar, T.RA[:, c:c + 128], T.II[:], 8 * (b_ - w_), T.PB[:, b_:b_ + 1], A.is_equal, A.mult, r="II PB%d" % b_, w="RA%d%d" % (b_, w_))
    v(V.tensor_copy, T.SDF[:], T.SDI[:], r="SDI", w="SDF")
    v(V.tensor_copy, T.NLF[:], T.NLI[:], r="NLI", w="NLF")
    for hf in range(2):
        mm(T.B4[:, 8 * hf:8 * hf + 8], T.SDF[:, 128 * hf:128 * hf + 128], T.IDF[0:8, 0:8], r="SDF IDF", w="B4sd", b="B4")
    for hf in range(2):
        mm(T.B4[:, 16 + 8 * hf:24 + 8 * hf], T.NLF[:, 128 * hf:128 * hf + 128], T.IDF[0:8, 0:8], r="NLF IDF", w="B4sd", b="B4")
    v(V.memset, T.ROW0[:], 0.0, w="ROW0")
    v(V.tensor_scalar, T.IG[:], T.IG[:], 4, None, A.arith_shift_right, r="IG", w="IG")
    v(V.tensor_scalar, T.KB[:], T.IG[:], 0, None, A.is_equal, r="IG", w="KB")
    v(V.tensor_scalar, T.KF[:], T.IG[:], 0, None, A.is_equal, r="IG", w="KF")
    v(V.tensor_scalar, T.IM[:], T.IM[:], 15, None, A.bitwise_and, r="IM", w="IM")
    v(V.tensor_scalar, T.ME[:], T.IM[:], 0, None, A.is_equal, r="IM", w="ME")
    v(V.tensor_copy, T.LS9[:], T.I9[:], r="I9a I9b I9c I9d", w="LS9")
    v(V.tensor_scalar, T.LK9[:], T.I9[:], 20, 19, A.mult, A.add, r="I9a I9b I9c I9d", w="LK9")
    v(V.tensor_copy, T.LU[:], T.IU[:], r="IU", w="LU")
    v(V.tensor_copy, T.SI[:], T.B4[:, 0:16], r="B4sd", w="SI", b="B4")
    v(V.tensor_copy, T.N0[:], T.B4[:, 16:32], r="B4sd", w="N0", b="B4")
    v(V.tensor_scalar, T.P15I[:, 0:1], T.IP[:, 0:1], 15, None, A.bitwise_and, r="IP", w="P15I")
    v(V.tensor_copy, T.P15[:], T.P15I[:, 0:1], r="P15I", w="P15")
    v(V.tensor_copy, T.IDB[:], T.IDF[:], r="IDF", w="IDB")

    def push1(ncol, nkey, first=None):
        if not first:
            v(V.tensor_tensor, T.T1[:], T.SI[:], T.SI[:], A.mult, r="SI", w="T1")
            v(V.tensor_scalar, T.U[:], ncol, 77, None, A.mult, r=nkey, w="U")
        v(V.tensor_scalar, T.S15[:], T.SI[:], 15, None, A.bitwise_and, r="SI", w="S15")
        if first:
            first()
        v(V.tensor_scalar, T.T2[:], T.T1[:], 5, None, A.arith_shift_right, r="T1", w="T2")
        v(V.tensor_tensor, T.U[:], T.U[:], T.SI[:], A.add, r="U SI", w="U")
        v(V.tensor_tensor, T.T1[:], T.T2[:], T.U[:], A.add, r="T2 U", w="T1")
        v(V.tensor_scalar, T.CI[:], T.T1[:], 1023, None, A.bitwise_and, r="T1", w="CI")
        v(V.tensor_tensor, T.EC[:], T.CI[:].indirect(T.LS9[:]), T.ME[:], A.mult, r="CI LS9 ME", w="EC")
        v(V.tensor_copy, T.RS[:], T.S15[:].indirect(T.LS9[:]), r="S15 LS9", w="RS")

    def push2(sl):
        for hf in range(2):
            mm(T.PG[:, 8 * hf:8 * hf + 8], T.EC[:, 144 * hf + sl:144 * hf + sl + 128], T.KF[:], r="EC KF", w="pC", b="PG0")
        for hf in range(2):
            mm(T.PG[:, 512 + 128 * hf:640 + 128 * hf], T.RS[:, 144 * hf + sl:144 * hf + sl + 128], T.IDB[:], r="RS IDB", w="pR", b="PG1")

    def push2a():
        v(V.tensor_copy, T.CL[:], T.PG[:, 0:16], r="pC", w="CL", b="PG0")
        v(V.tensor_scalar, T.MK[:], T.PG[:, 512:768], T.P15[:], None, A.is_equal, r="pR P15", w="MK", b="PG1")

    def push2b(ls):
        v(V.tensor_tensor, T.MM[:], T[ls][:].indirect(T.CL[:]), T.MK[:], A.mult, r=ls + " CL MK", w="MM")

    lwb = {0: (T.B5, 16, "B5"), 1: (T.PG, 1024, "PG2")}

    def push2w(k_=1):
        B, c, bk = lwb[k_]
        for hf in range(2):
            mm(B[:, c + 8 * hf:c + 8 + 8 * hf], T.MM[:, 128 * hf:128 * hf + 128], T.KF[:], r="MM KF", w="pW", b=bk)

    def push2f():
        mm(T.B5[:, 256:512], T.ROW0[:], T.MM[:], r="MM ROW0", w="pF", b="B5")

    def push3(k_=1):
        B, c, bk = lwb[k_]
        v(V.tensor_copy, T.LW[:], B[:, c:c + 16], r="pW", w="LW", b=bk)

    def push3f(t):
        act(T.LF[:, 256 * t:256 * t + 256], T.B5[:, 256:512], r="pF", w="LF%d" % t, b="B5")

    def push4():
        v(V.tensor_tensor, T.EL[:], T.LW[:].indirect(T.LU[:]), T.ME[:, 0:256], A.mult, r="LW LU ME", w="EL")
        for hf in range(2):
            mm(T.B5[:, 8 * hf:8 * hf + 8], T.EL[:, 128 * hf:128 * hf + 128], T.KF[:], r="EL KF", w="pL", b="B5")

    v(V.tensor_copy, T.W2[:, 0:256], T.WI[:], r="WIa WIb", w="W20")
    push1(T.N0[:], "N0")

    def rearr(t, b_):
        w2 = 256 * t
        out, bk = (T.B4[:, 128:256], "B4") if b_ == 0 else (T.PG[:, 1792:1920], "PG3")
        for w_ in range(2):
            c = 128 * (2 * b_ + w_)
            mm(out, T.RA[:, c:c + 128], T.W2[:, w2 + w_:w2 + 256:2], w_ == 0, w_ == 1, r="W2%d RA%d%d" % (t, b_, w_), w="pH%d" % b_, b=bk)

    def lists(b_):
        src, bk = (T.B4[:, 128:256], "B4") if b_ == 0 else (T.PG[:, 1792:1920], "PG3")
        v(V.tensor_copy, T.LH[:, 128 * b_:128 * b_ + 128], src, r="pH%d" % b_, w="LH%d" % b_, b=bk)

    rearr(0, 0)
    rearr(0, 1)
    push2(16)
    lists(0)
    act(T.KN[:], T.KB[:], scale=-1.0, r="KB", w="KN")
    act(T.K2[:], T.KB[:], scale=2.0, r="KB", w="K2")
    act(T.NIB[:], T.IDB[:], scale=-1.0, r="IDB", w="NIB")
    act(T.ROW0[:, 0:128:16], T.KF[:], r="KF", w="ROW0")
    cpk = ["CP"] * 5
    for k_ in (1, 2, 3, 0, 4):
        rr = k_ % 4
        for h in HS[k_ // 4:]:
            for j in (rr, rr - h):
                if 0 <= j < h:
                    key, c = "CP%d%d" % (k_, h), 160 * k_ + BASE[h] + j
                    act(T.CP[:, c:160 * k_ + 160:20], T.KN[:], r="KN CP", w=key)
                    cpk[k_] += " " + key
    act(T.SH[:, 768:1024], T.W2[:, 0:256], scale=0.0, r="W20", w="SH3")
    act(T.SH[:, 1536:1792], T.W2[:, 0:256], scale=0.0, r="W20", w="SH6")
    act(T.ONEF[:], T.IDF[:], F.Identity, scale=0.0, bias=1.0, r="IDF", w="ONEF")
    act(T.NEG[:], T.W2[:, 0:256], F.Identity, scale=0.0, bias=-128.0, r="W20", w="NEG")
    push2a()
    send("LS", prv, T.LSN[:], T.LS[:], r="LS")

    def first0():
        lists(1)

    v(V.tensor_copy, T.THF[:], T.THI[:], r="THI", w="THF")
    v(V.tensor_scalar, T.DB[:], T.I20[:], 0, None, A.is_equal, r="I20", w="DB")
    v(V.tensor_scalar, T.BC[:], T.THF[:], -1, None, A.mult, r="THF", w="BC")

    shk = "SH3 SH6 SHf SHg " + " ".join("SA%d SB%d" % (h, h) for h in (8, 5, 3, 2, 1, 0))

    def n1(ncol, nkey):
        v(V.tensor_scalar, T.N1[:], ncol, 1, 16, A.add, A.min, r=nkey, w="N1")

    def thr():
        for h in HS:
            e = BASE[h] + h - 1
            v(V.tensor_scalar, T.THR[:, e:320:20], T.N1[:], 0.5 - 2 * h, 0.0, A.add, A.min, r="N1 THR", w="THR%d" % e)
    thk = "THR THR0 " + " ".join("THR%d" % (BASE[h] + h - 1) for h in HS)

    def bound():
        v(V.tensor_scalar, T.RB[:], T.DB[:], T.BC[:], None, A.mult, r="DB BC", w="RB")

    def build_sh(t):
        for h in (8, 5, 3, 2, 1, 0):
            c, d = 256 * SLOT[h], 17 - h
            dma("sh", T.SH[d:128, c:c + 256], T.W2R[0:128 - d, 256 * t:256 * t + 256], r="W2R%d" % t, w="SA%d" % h)
            dma("sh", T.SH[0:d, c:c + 256], T.W2R[128 - d:128, 256 * t:256 * t + 256], r="W2R%d" % t, w="SB%d" % h)
        dma("sh2", T.SH[17:128:16, 1280:1536], T.LFR[0:112:16, 256 * t:256 * t + 256], r="LFR%d SA0 SB0" % t, w="SHf")
        dma("sh2", T.SH[1:2, 1280:1536], T.LFR[112:113, 256 * t:256 * t + 256], r="LFR%d SA0 SB0" % t, w="SHg")

    def idx(h, j):
        return PAIRS.index((h, j))

    def pd(hf, lo, hi):
        return (T.PD0 if hf == 0 else T.PD1)[:, lo:hi]

    def place(hf, h, j):
        return (T.PD0 if hf == 0 else T.PD1)[:, BASE[h] + j:160:20]

    def bulk(t, mid, hole):
        PGK = "PG0 PG1 PG2 PG3"
        v(V.tensor_copy, T.GL[:, 1024:1536], T.X[:, 0:4096].indirect(T.LH[:, 64:96]), r="XA XB LH0", w="GLd R0d")
        for c, k_ in ((0, "c"), (512, "a"), (1536, "b")):
            act(T.GL[:, c:c + 512], T.X[:, 0:4096].indirect(T.LH[:, c // 16:c // 16 + 32]), r="XA XB LH0", w="GL%s R0%s" % (k_, k_))
        for b_ in range(2):
            if b_ == 1:
                mid()
            c, k_ = 512 * b_, "a" if b_ else "c"
            mm(T.PG[:, c:c + 512], T.IDB[:], T.GL[:, c:c + 512], r="IDB GL%s R0%s" % (k_, k_), w="pg", b="PG%d" % b_)
            c, k_ = 1024 + 512 * b_, "b" if b_ else "d"
            for j in range(1, 6):
                mm(T.PG[:, c + j:c + 512:8], T.IDB[:], T.GL[:, c + j:c + 512:8], r="IDB GL%s" % k_, w="pg", b="PG%d" % (2 + b_))
        act(T.GH[:, 0:1024], T.X[:, 0:4096].indirect(T.LH[:, 128:192]), r="XA XB LH1", w="GHa")
        act(T.GH[:, 1024:2048], T.X[:, 0:4096].indirect(T.LH[:, 192:256]), r="XA XB LH1", w="GHb")
        hole()

        def low(hf, j):
            gl = T.GL[:, 1024 * hf + j:1024 * hf + 1024:8]
            key = ("R0" if j == 0 else "GL") + "ab"[hf]
            if j < 4:
                k_ = 4 if hf == 1 and j == 0 else j
                mm(pd(hf, 0, 160), gl, T.CP[:, 160 * k_:160 * k_ + 160], False, False, r=key + " " + cpk[k_], w="pd%d" % hf, b="PD%d" % hf)
                return
            for h in HS:
                if h > j and not (h == 8 and hf == 1):
                    mm(place(hf, h, j), gl, T.KN[:], False, False, r=key + " KN", w="pd%d" % hf, b="PD%d" % hf)

        def high(hf, rr):
            for h in HS:
                j = rr - h
                if 0 <= j < h and not (h == 8 and hf == 1 and j not in MAXED):
                    src, key = (T.GL, "GL") if rr < 8 else (T.GH, "GH")
                    o = 1024 * hf + rr % 8
                    mm(place(hf, h, j), src[:, o:1024 * hf + 1024:8], T.KN[:], False, False, r=key + "ab"[hf] + " KN", w="pd%d" % hf, b="PD%d" % hf)

        def add(hf, h, j, last=False):
            o = place(hf, h, j)
            if h == 8:
                if hf == 0:
                    mm(o, T.D8[:, j:1024:8], T.K2[:], False, last, r="K2 D8a D8b" + (" D8j" if j == 0 else ""), w="pd0", b="PD0")
                else:
                    mm(o, T.D8[:, 1024 + 128 * j:1152 + 128 * j], T.K2[:] if j in MAXED else T.KB[:], False, last,
                       r="K2 D8y%d" % j if j in MAXED else "KB D8x%d" % min(j, 4), w="pd1", b="PD1")
            else:
                c = 256 * idx(h, j) + 128 * hf
                mm(o, T.DL[:, c:c + 128], T.K2[:], False, last, r="K2 DL%d%d" % (h, j), w="pd%d" % hf, b="PD%d" % hf)

        def pair(h, j):
            c = 256 * idx(h, j)
            if j == 0:
                i0, i1, key = T.PG[:, h:2048:8], T.GL[:, 0:2048:8], "R0a R0b"
            elif j + h < 8:
                i0, i1, key = T.PG[:, j:2048:8], T.GL[:, j + h:2048:8], "GLa GLb"
            else:
                i0, i1, key = T.PG[:, j:2048:8], T.GH[:, j + h - 8:2048:8], "GHa GHb"
            v(V.tensor_tensor, T.DL[:, c:c + 256], i0, i1, A.max, r="pg " + key, w="DL%d%d" % (h, j), b=PGK)

        def sizes(js, B, bk):
            n = 128 * len(js)
            for q_, j in enumerate(js):
                mm(B[:, 128 * q_:128 * q_ + 128], T.IDB[:], T.GL[:, 1024 + j:2048:8], True, False, r="IDB %sb" % ("R0" if j == 0 else "GL"), b=bk)
                mm(B[:, 128 * q_:128 * q_ + 128], T.NIB[:], T.GH[:, 1024 + j:2048:8], False, True, r="NIB GHb", w="pB" + bk, b=bk)
            act(T.D8[:, 1024 + 128 * js[0]:1024 + 128 * js[0] + n], B[:, 0:n], F.Abs, r="pB" + bk, w="D8x%d" % js[0], b=bk)

        def row0():
            act(T.GL[:, 0:2048:8], T.X[:, 0:4096].indirect(T.LLU[:]), r="XA XB LLU GLa GLb", w="R0a R0b R0c R0d")

        early = ((2, 1), (3, 1), (3, 2), (5, 1), (5, 2))
        for h, j in early:
            pair(h, j)
        v(V.tensor_tensor, T.D8[:, 0:512], T.PG[:, 0:512], T.GH[:, 0:512], A.max, r="pg GHa", w="D8a", b="PG0")
        if t > 0:
            v(V.tensor_copy, T.LLU[:], T.MNR[:, 32 * (t - 1) + 16:32 * t], r="MNR%d" % (t - 1), w="LLU")
            v(V.tensor_scalar, T.S5[:], T.MNR[:, 32 * (t - 1):32 * (t - 1) + 16], 5, None, A.mult, r="MNR%d" % (t - 1), w="S5")
            row0()
        else:
            push2b("LS")
        for hf in range(2):
            if hf == 1:
                if t == 0:
                    push2w(0)
                    push3(0)
                    push4()
                v(V.tensor_tensor, T.D8[:, 512:1024], T.PG[:, 512:1024], T.GH[:, 512:1024], A.max, r="pg GHa", w="D8b", b="PG1")
            mm(pd(hf, 0, 160), T.ONE[:], T.RB[:], True, False, r="ONE RB", w="pd%d" % hf, b="PD%d" % hf)
            for rr in range(1, 8):
                low(hf, rr)
                if rr > 3:
                    high(hf, rr)
        if t == 0:
            v(V.tensor_copy, T.LLU[:], T.B5[:, 0:16], r="pL", w="LLU", b="B5")
            row0()
        sizes((4, 5, 6, 7), T.B4, "B4")
        sizes((0,), T.B5, "B5")
        for j in MAXED:
            v(V.tensor_tensor, T.D8[:, 1024 + 128 * j:1152 + 128 * j], T.PG[:, 1024 + j:2048:8], T.GH[:, 1024 + j:2048:8], A.max, r="pg GHb", w="D8y%d" % j, b="PG2 PG3")
        for rr in range(8, 16):
            high(0, rr)
        for h, j in early:
            for hf in range(2):
                add(hf, h, j)
        for j in range(1, 8):
            add(0, 8, j)
        for rr in (8, 9) + tuple(8 + j for j in MAXED if j > 1):
            high(1, rr)
        for h, j in ((5, 3), (5, 4)):
            pair(h, j)
            for hf in range(2):
                add(hf, h, j)
        for hf in range(2):
            low(hf, 0)
        v(V.tensor_tensor, T.D8[:, 0:1024:8], T.GL[:, 0:1024:8], T.GH[:, 0:1024:8], A.max, r="R0a GHa D8a D8b", w="D8j")
        add(0, 8, 0)
        for j in range(1, 8):
            add(1, 8, j)
        add(1, 8, 0)
        for h in (5, 3, 2, 1):
            pair(h, 0)
            for hf in range(2):
                add(hf, h, 0, h == 1)
        if t == 0:
            push2f()
            push3f(0)
            send("LF0", nxt, T.LFR[:, 0:256], T.LF[:, 0:256], r="LF0")
        v(V.tensor_tensor_scan, T.ZC[:], T.ZR[:], T.GL[:], 0.0, A.mult, A.max, r="ZR GLa GLb R0a R0b", w="ZC")
        act(T.ZC[:, 5:2048:8], T.GL[:, 0:2048:8], r="R0a R0b ZC", w="ZC5")

    def decode(t):
        last = t == TV - 1
        rs = 16 if last else 0
        m1 = 288 * t
        halves = ((0, T.B4, "B4", 0), (1, T.B5, "B5", 160))
        for hf, B, bk, c in halves:
            v(V.tensor_tensor_scan, B[:, 0:160], T.D0[:], pd(hf, 0, 160), 0.0, A.mult, A.max, r="pd%d %s" % (hf, d0k), w="s1%d" % hf, b="PD%d %s" % (hf, bk))
        for hf, B, bk, c in halves:
            v(V.tensor_tensor, T.E[:, c:c + 160], B[:, 0:160], T.THR[:, c:c + 160], A.is_gt, r="s1%d %s" % (hf, thk), w="E%d" % hf, b=bk)
        for hf, B, bk, c in halves:
            v(V.tensor_tensor_scan, T.SC2[:, c:c + 160], T.E[:, c:c + 160], T.C2[:], 0.0, A.mult, A.add, r="E%d %s" % (hf, c2k), w="SC%d" % hf)
        v(V.tensor_tensor, T.EK[:], T.SC2[:].indirect(T.LK9[:]), T.ME[:], A.mult, r="SC0 SC1 LK9 ME", w="EK")
        mm(T.PG[:, 0:16], T.IDB[:], T.B8[:], True, False, r="IDB B8", w="p1", b="PG0")
        for hf in range(2):
            mm(T.PG[:, 8 * hf:8 * hf + 8], T.EK[:, 144 * hf + 16:144 * hf + 144], T.KB[:], False, hf == 1, r="EK KB", w="p1", b="PG0")
        for hf in range(2):
            mm(T.PG[:, 512 + 8 * hf:520 + 8 * hf], T.EK[:, 144 * hf + rs:144 * hf + rs + 128], T.K256[:], r="EK K256", w="p2", b="PG1")
        kap = T.SC2[:, 19:320:20]
        v(V.tensor_scalar, T.NH[:], kap, 5, None, A.is_equal, r="SC0 SC1", w="NH")
        v(V.tensor_scalar, T.DU[:], T.NH[:], 4096, None, A.mult, r="NH", w="DU")
        v(V.tensor_scalar, T.H1[:], T.NH[:], -6, 1, A.mult, A.add, r="NH", w="H1")
        v(V.tensor_tensor, T.S5[:], T.S5[:], T.NH[:], A.mult, r="S5 NH", w="S5")
        v(V.tensor_copy, T.L1[:], T.PG[:, 0:16], r="p1", w="L1", b="PG0")
        v(V.tensor_tensor, T.H[:], T.H1[:], kap, A.add, r="H1 SC0 SC1", w="H")
        v(V.tensor_copy, T.M1S[:, m1:m1 + 128], T.ZC[:].indirect(T.L1[:, 0:8]), r="ZC ZC5 L1", w="Za")
        act(T.M1S[:, m1 + 128:m1 + 256], T.ZC[:].indirect(T.L1[:, 8:16]), r="ZC ZC5 L1", w="Zb")
        act(T.M1S[:, m1 + 256:m1 + 272], T.PG[:, 512:528], r="p2", w="Zc", b="PG1")
        for hf in range(2):
            mm(T.PG[:, 1024 + 8 * hf:1032 + 8 * hf], T.M1S[:, m1 + 128 * hf:m1 + 128 * hf + 128], T.WTB[:], r="Z%s WTB" % "ab"[hf], w="pt", b="PG2")
        mm(T.PG[:, 1536:1552], T.IDB[:], T.B16[:], True, False, r="IDB B16", w="p3", b="PG3")
        v(V.tensor_tensor, T.AD[:], T.S5[:], T.H[:], A.add, r="S5 H", w="AD")
        v(V.tensor_tensor, T.NP[:], T.N1[:], T.H[:], A.subtract, r="N1 H", w="NP")
        v(V.tensor_tensor, T.SUM[:], T.PG[:, 1024:1040], T.AD[:], A.add, r="pt AD", w="SUM", b="PG2")
        if last:
            v(V.tensor_copy, T.M1S[:, m1 + 272:m1 + 288], T.NP[:], r="NP", w="Zd")
        else:
            v(V.tensor_copy, T.M1S[:, m1 + 272:m1 + 288], T.NP[:].indirect(T.ROT[:, 0:1]), r="NP ROT", w="Zd")
        v(V.tensor_scalar, T.V15[:], T.SUM[:], 15, None, A.bitwise_and, r="SUM", w="V15")
        v(V.tensor_tensor, T.VV[:], T.V15[:], T.DU[:], A.max, r="V15 DU", w="VV")
        v(V.tensor_tensor, T.EV[:], T.VV[:].indirect(T.LU[:]), T.ME[:, 0:256], A.mult, r="VV LU ME", w="EV")
        for hf in range(2):
            mm(T.PG[:, 1536 + 8 * hf:1544 + 8 * hf], T.EV[:, 128 * hf:128 * hf + 128], T.KB[:], False, hf == 1, r="EV KB", w="p3", b="PG3")
        v(V.tensor_scalar, T.SI[:], T.SUM[:], 4095, None, A.bitwise_and, r="SUM", w="SI")
        if not last:
            v(V.tensor_scalar, T.U[:], T.NP[:], 77, None, A.mult, r="NP", w="U")
            v(V.tensor_tensor, T.T1[:], T.SI[:], T.SI[:], A.mult, r="SI", w="T1")
        v(V.tensor_copy, T.MLS[:, 16 * t:16 * t + 16], T.PG[:, 1536:1552], r="p3", w="MLS", b="PG3")
        send("M1%d" % t, nxt, T.M1R[:, m1:m1 + 288], T.M1S[:, m1:m1 + 288], r="Za Zb Zc Zd")
        send("ML%d" % t, nxt, T.MLR[:, 16 * t:16 * t + 16], T.MLS[:, 16 * t:16 * t + 16], r="MLS")

    def xupdate(t, cols, lo, e0, e1, ck, xk):
        win = T.X[:, lo:8192]
        v(V.tensor_tensor, T.XT[:, e0:e1], win.indirect(cols), T.M1R[:, 288 * t + e0:288 * t + e1], A.add, r="M1R%d %s %s" % (t, ck, xk), w="XT")
        v(V.tensor_scalar, T.XU[:, e0:e1], T.XT[:, e0:e1], 0.5, 127.75, A.mult, A.add, r="XT", w="XU")
        v(V.tensor_tensor, win.indirect(cols), T.XU[:, e0:e1], T.NEG[:, e0:e1], A.add, r="XU NEG " + ck, w=xk)

    def first():
        bound()
        v(V.memset, T.ONE[:], 1.0, w="ONE")
        v(V.memset, T.THR[:], -1.0, w="THR")
        v(V.memset, T.THR[:, 0:320:20], 1000.0, r="THR", w="THR0")
        n1(T.N0[:], "N0")
        thr()
        v(V.memset, T.ZR[:, 0:2048:8], 0.0, r="ZR", w="ZR")
        v(V.tensor_copy, T.WTF[:], T.WTI[:], r="WTI", w="WTF")
        v(V.tensor_scalar, T.BI[:], T.IK[:], T.P15[:], None, A.add, r="IK P15", w="BI")
        act(T.WTB[:], T.KB[:], scale=T.WTF[:], r="KB WTF", w="WTB")
        act(T.K256[:], T.KB[:], scale=256.0, r="KB", w="K256")
        act(T.B8[:], T.BI[:], scale=8.0, r="BI", w="B8")
        act(T.B16[:], T.BI[:], scale=16.0, r="BI", w="B16")
        v(V.tensor_scalar, T.S5[:], T.SI[:], 5, None, A.mult, r="SI", w="S5")

    def rot_list():
        v(V.tensor_scalar, T.P15I[:, 2:3], T.P15I[:, 0:1], 8, None, A.bitwise_and, r="P15I", w="P15c")
        v(V.tensor_scalar, T.P15I[:, 3:4], T.P15I[:, 0:1], -1, None, A.add, r="P15I", w="P15d")
        v(V.tensor_scalar, T.P15I[:, 3:4], T.P15I[:, 3:4], 7, None, A.bitwise_and, r="P15d", w="P15d")
        v(V.tensor_tensor, T.P15I[:, 2:3], T.P15I[:, 2:3], T.P15I[:, 3:4], A.add, r="P15c P15d", w="P15c")
        v(V.tensor_copy, T.ROT[:, 0:1], T.P15I[:, 2:3], r="P15c", w="ROT")

    for t in range(TV):
        if t < TV - 1:
            send("W2%d" % t, nxt, T.W2R[:, 256 * t:256 * t + 256], T.W2[:, 256 * t:256 * t + 256], r="W2%d" % t)
            build_sh(t)
        else:
            for h in (8, 5, 3, 2, 1, 0):
                c = 256 * SLOT[h]
                dma("sh", T.SH[0:128 - h, c:c + 256], T.W2[h:128, 1024:1280], r="W24", w="SA%d SB%d" % (h, h))
            dma("sh2", T.SH[0:128:16, 1280:1536], T.LFR[0:128:16, 1024:1280], r="LFR4 SA0 SB0", w="SHf SHg")
        bulk(t, *((first0, first) if t == 0 else (mid, hole)))
        if t == 0:
            consts_scan()
            rot_list()
        decode(t)
        if t == TV - 1:
            break
        u = t + 1
        m1 = 288 * t
        push1(T.NP[:], "NP", lambda: v(V.tensor_reduce, T.NS[:], T.NH[:], AxisListType.X, A.add, r="NH", w="NS"))
        v(V.tensor_copy, T.MNS[:, 32 * t:32 * t + 16], T.SI[:].indirect(T.ROT[:, 0:1]), r="SI ROT", w="MNa")
        v(V.tensor_tensor, T.KBI[:], T.M1R[:, m1 + 256:m1 + 272], T.BI[:], A.add, r="M1R%d BI" % t, w="KBI")
        v(V.tensor_copy, T.L2[:], T.KBI[:], r="KBI", w="L2")
        act(T.W2[:, 256 * u:256 * u + 256], T.SH[:].indirect(T.L2[:]), r="L2 " + shk, w="W2%d" % u)
        mm(T.PG[:, 256:257], T.ONEF[:], T.NS[:], r="ONEF NS", w="pA", b="PG0")
        push2(0)
        rearr(u, 0)
        push2a()
        push2b("LSN")
        push2w()
        rearr(u, 1)
        push2f()
        v(V.tensor_scalar, T.AI[:], T.PG[:, 256:257], -1, 2048, A.mult, A.add, r="pA", w="AI", b="PG0")
        xupdate(t, T.MLR[:, 16 * t:16 * t + 16], 0, 0, 256, "MLR%d" % t, "XA XB XD")
        lists(0)

        push3()

        def mid(m1=m1):
            lists(1)
            push4()
            v(V.tensor_scalar, T.AJ[:], T.AI[:], 15, None, A.bitwise_and, r="AI", w="AJ")
            n1(T.M1R[:, m1 + 272:m1 + 288], "M1R%d" % (m1 // 288))

        def hole(t=t, u=u):
            v(V.tensor_copy, T.MNS[:, 32 * t + 16:32 * t + 32], T.B5[:, 0:16], r="pL", w="MNb", b="B5")
            send("MN%d" % t, nxt, T.MNR[:, 32 * t:32 * t + 32], T.MNS[:, 32 * t:32 * t + 32], r="MNa MNb")
            push3f(u)
            send("LF%d" % u, nx2 if u < 4 else nxt, T.LFR[:, 256 * u:256 * u + 256], T.LF[:, 256 * u:256 * u + 256], r="LF%d" % u)
            v(V.tensor_scalar, T.BC[:], T.AJ[:], T.THF[:], -1, A.add, A.mult, r="AJ THF", w="BC")
            thr()
            bound()

    v(V.tensor_copy, T.SF[:], T.SI[:], r="SI", w="SF")
    v(V.tensor_tensor, T.KBI[:], T.M1S[:, 4 * 288 + 256:4 * 288 + 272], T.BI[:], A.add, r="Zc BI", w="KBI")
    v(V.tensor_copy, T.L2[:], T.KBI[:], r="KBI", w="L2")
    v(V.tensor_copy, T.RS[:], T.NP[:].indirect(T.LS9[:]), r="NP LS9", w="RS")
    for hf in range(2):
        mm(T.PG[:, 512 + 128 * hf:640 + 128 * hf], T.RS[:, 144 * hf + 16:144 * hf + 144], T.IDB[:], r="RS IDB", w="pR", b="PG1")
    for hf in range(2):
        mm(T.PG[0:8, 128 * hf:128 * hf + 128], T.NP[:, 8 * hf:8 * hf + 8], T.IDF[:], r="NP IDF", w="pN", b="PG0")
    for hf in range(2):
        mm(T.PG[0:8, 1024 + 128 * hf:1152 + 128 * hf], T.SF[:, 8 * hf:8 * hf + 8], T.IDF[:], r="SF IDF", w="pS", b="PG2")
    v(V.tensor_scalar, T.MK[:], T.PG[:, 512:768], T.P15[:], None, A.is_gt, r="pR P15", w="MK", b="PG1")
    v(V.tensor_tensor, T.YW[:], T.SH[:].indirect(T.L2[:]), T.MK[:], A.mult, r="L2 MK " + shk, w="YW")
    dma("oyw", T.yw[:], T.YW[:], r="YW")
    xupdate(4, T.MLR[:, 64:72], 0, 0, 128, "MLR4", "XA XB XD")
    dma("oyx", T.yx[:, 0:2048], T.X[:, 0:2048], r="XA")
    v(V.tensor_scalar, T.CL[:, 0:8], T.MLR[:, 72:80], -2048, None, A.add, r="MLR4", w="CL")
    xupdate(4, T.CL[:, 0:8], 2048, 128, 256, "CL", "XB XD")
    dma("oyx", T.yx[:, 2048:4096], T.X[:, 2048:4096], r="XB")
    act(T.YN[:], T.PG[0:8, 0:256], r="pN", w="YN", b="PG0")
    act(T.YS[:], T.PG[0:8, 1024:1280], r="pS", w="YS", b="PG2")
    dma("oyn", T.yn[:], T.YN[:], r="YN")
    dma("oyn", T.ys[:], T.YS[:], r="YS")
    for sem, n in tot.items():
        if known["g"].get(sem, 0) < n:
            g.wait_ge(T.sem[sem], n)
